import numpy as np
import ml_dtypes


def mxq(x, axis, fmt="e4m3"):
    dtype, down = {"e4m3": (ml_dtypes.float8_e4m3fn, 7), "e5m2": (ml_dtypes.float8_e5m2, 14)}[fmt]
    v = np.moveaxis(np.asarray(x, np.float32).astype(ml_dtypes.bfloat16).astype(np.float64), axis, -1)
    blocks = v.reshape(v.shape[:-1] + (-1, 32))
    amax = np.abs(blocks).max(-1, keepdims=True)
    byte = np.maximum(np.where(amax > 0, np.frexp(amax)[1] - 1 + 127, 0) - down, 1)
    scale = np.exp2(byte - 127.0)
    codes = (blocks / scale).astype(np.float32).astype(dtype).astype(np.float64)
    return np.moveaxis((codes * scale).reshape(v.shape), -1, axis)


WIDE = False


def mx_kscale(k):
    if not WIDE:
        return np.ones(k)
    levels = np.array([10, -10, 5, -5, 0])
    if k % 512:
        return np.exp2(np.random.permutation(np.resize(levels, k // 32))).repeat(32)
    a = np.empty((k // 512, 16))
    for p in range(k // 512):
        a[p, :8] = np.random.permutation(np.resize(levels, 8))
        for g in range(8):
            far = levels[np.abs(levels - a[p, g]) >= 10]
            a[p, g + 8] = far[np.random.randint(len(far))]
    return np.exp2(a.ravel()).repeat(32)


def f64(x):
    return np.asarray(x).astype(np.float64)


def striped(idx):
    return np.tile(idx.reshape(-1, 16).T, (8, 1)).astype(np.uint16)


def unstriped(offs):
    return offs[:16].T.reshape(-1).astype(np.int64)


E2M1 = np.array([0.0, 0.5, 1.0, 1.5, 2.0, 3.0, 4.0, 6.0, -0.0, -0.5, -1.0, -1.5, -2.0, -3.0, -4.0, -6.0])


def pack_weight(w, fmt):
    k, n = w.shape
    w = f64(np.asarray(w, np.float32).astype(ml_dtypes.bfloat16)).reshape(k // 32, 32, n)
    amax = np.abs(w).max(1)
    if fmt == "e4m3":
        byte = np.frexp(amax)[1] - 1 + 127 - 7
    else:
        mant, ex = np.frexp(amax / 6.0)
        byte = np.where(mant > 0.5, ex, ex - 1) + 127
    byte = np.clip(np.where(amax > 0, byte, 1), 1, 254)
    scaled = (w * np.exp2(127.0 - byte)[:, None, :]).reshape(k, n).astype(np.float32)
    by_word = np.ascontiguousarray(scaled.reshape(k // 512, 128, 4, n).transpose(0, 1, 3, 2))
    if fmt == "e4m3":
        words = by_word.astype(ml_dtypes.float8_e4m3fn).view(np.uint8)
    else:
        c = by_word.astype(ml_dtypes.float4_e2m1fn).view(np.uint8) & 0xF
        words = (c[..., 0::2] | (c[..., 1::2] << 4)).reshape(k // 512, 128, 2 * n)
    return np.ascontiguousarray(words), np.ascontiguousarray(byte.astype(np.uint8).reshape(k // 512, 16, n))


def unpack_weight(words, scales, fmt):
    g, _, n = scales.shape
    words = np.ascontiguousarray(words).reshape(g, 128, n, -1)
    if fmt == "e4m3":
        vals = words.view(ml_dtypes.float8_e4m3fn).astype(np.float64)
    else:
        nib = np.empty((g, 128, n, 4), np.uint8)
        nib[..., 0::2] = words & 0xF
        nib[..., 1::2] = words >> 4
        vals = E2M1[nib]
    vals = vals * np.repeat(np.exp2(scales.astype(np.float64) - 127.0), 8, axis=1)[..., None]
    return vals.transpose(0, 1, 3, 2).reshape(g * 512, n)


def relu2(v):
    return np.maximum(v, 0.0) ** 2


K, T, E, C, H, N = 2048, 512, 6, 128, 512, 384
R = 4


def by_expert(wq, xq):
    return np.concatenate([wq[e].T @ xq[:, e * C:(e + 1) * C] for e in range(E)], axis=1)


def setup_inputs():
    n = np.random.standard_normal
    s = mx_kscale(K)[:, None]
    u = mx_kscale(H)
    slot_token = np.concatenate([r * (T // R) + np.random.permutation(T // R)[:C // R] for e in range(E) for r in range(R)])
    w1 = [pack_weight(m, "e2m1") for m in n((E, K, H)) / np.sqrt(K) / s[None] * u[None, None, :]]
    w2 = [pack_weight(m, "e2m1") for m in n((E, H, N)) / np.sqrt(H) / u[None, :, None] ** 2]
    return {
        "xT": (n((K, T)) * s).astype(np.float32),
        "w1_words": np.stack([m[0] for m in w1]),
        "w1_scales": np.stack([m[1] for m in w1]),
        "w2_words": np.stack([m[0] for m in w2]),
        "w2_scales": np.stack([m[1] for m in w2]),
        "offs": striped(slot_token),
    }


def reference(xT, w1_words, w1_scales, w2_words, w2_scales, offs):
    idx = unstriped(offs)
    w1 = np.stack([unpack_weight(w1_words[e], w1_scales[e], "e2m1") for e in range(E)])
    w2 = np.stack([unpack_weight(w2_words[e], w2_scales[e], "e2m1") for e in range(E)])
    xq = mxq(f64(xT)[:, idx], 0, "e4m3")
    h = relu2(by_expert(w1, xq))
    y = by_expert(w2, mxq(h, 0, "e4m3"))
    return y.reshape(N, E, R, C // R).transpose(0, 2, 1, 3).reshape(N, E * C)

@@ -1,0 +1,243 @@
+from contextlib import ExitStack
+
+import concourse.mybir as mybir
+from concourse.masks import make_identity
+
+K, T, E, C, H, N, R = 2048, 512, 6, 128, 512, 384, 4
+P = 128
+S = K // 512
+SLOTS = E * C
+FLOPS = 2 * SLOTS * (K * H + H * N)
+
+F32 = mybir.dt.float32
+BF16 = mybir.dt.bfloat16
+U32 = mybir.dt.uint32
+I32 = mybir.dt.int32
+U16 = mybir.dt.uint16
+U8 = mybir.dt.uint8
+E4M3 = mybir.dt.float8_e4m3fn_x4
+E2M1 = mybir.dt.float4_e2m1fn_x4
+RELU = mybir.ActivationFunctionType.Relu
+SQUARE = mybir.ActivationFunctionType.Square
+
+
+def tile_moe_eps_mlp_relu2_kernel(
+    tc, xT, w1_words, w1_scales, w2_words, w2_scales, offs, out
+):
+    nc = tc.nc
+    with ExitStack() as ctx:
+        keep = ctx.enter_context(tc.tile_pool(name="keep", bufs=1))
+        work = ctx.enter_context(tc.tile_pool(name="work", bufs=3))
+        psum_a = ctx.enter_context(tc.psum_pool(name="psum_a", bufs=4))
+        psum_t = ctx.enter_context(tc.psum_pool(name="psum_t", bufs=2))
+        psum_y = ctx.enter_context(tc.psum_pool(name="psum_y", bufs=2))
+
+        offsets = keep.tile([P, SLOTS // 16], U16, name="offsets")
+        x = [keep.tile([P, 4, T], F32, name=f"x{s}") for s in range(S)]
+        xg = [keep.tile([P, T, 4], BF16, name=f"xg{s}", align_bytes=64) for s in range(S)]
+        codes = [keep.tile([P, T], U32, name=f"codes{s}", align_bytes=64) for s in range(S)]
+        scales = [keep.tile([P, T], U8, name=f"scales{i}", align_bytes=64) for i in range(3)]
+        gcodes = [keep.tile([P, SLOTS], U32, name=f"gcodes{s}", align_bytes=64) for s in range(S)]
+        gscales = [keep.tile([P, SLOTS], U8, name=f"gscales{s}", align_bytes=64) for s in range(S)]
+        w1 = [keep.tile([P, S, 2 * H], U8, name=f"w1_{e}", align_bytes=64) for e in range(E)]
+        w1s = keep.tile([P, E * S, H], U8, name="w1s", align_bytes=64)
+        w2 = keep.tile([P, E, 2 * N], U8, name="w2", align_bytes=64)
+        w2s = keep.tile([P, E, N], U8, name="w2s", align_bytes=64)
+        y = keep.tile([P, N // P, R, E, C // R], F32, name="y", align_bytes=64)
+        ident = keep.tile([P, P], F32, name="ident", align_bytes=64)
+
+        def load_x(s, c0, c1):
+            rows = xT[512 * s : 512 * (s + 1), c0:c1].rearrange("(p j) w -> p j w", j=4)
+            nc.sync.dma_start(out=x[s][:, :, c0:c1], in_=rows)
+
+        load_x(0, 0, 256)
+        nc.sync.dma_start(offsets[:], offs)
+        load_x(0, 256, 512)
+        load_x(1, 0, T)
+        load_x(2, 0, T)
+        load_x(3, 0, T)
+
+        nc.vector.memset(w1s[:].rearrange("p a i -> p (a i)").bitcast(I32), 0)
+        for plane in scales + [gscales[1]]:
+            nc.gpsimd.memset(plane[:], 0)
+        nc.gpsimd.memset(w2s[:].rearrange("p a i -> p (a i)").bitcast(I32), 0)
+
+        def load_w1s():
+            for r in range(4):
+                nc.sync.dma_start(
+                    out=w1s[r:P:32, :, :].bitcast(I32),
+                    in_=w1_scales.rearrange("e s (b r) i -> r b (e s) i", r=4)[r].bitcast(I32),
+                )
+
+        def load_w1(e):
+            nc.sync.dma_start(
+                out=w1[e][:].bitcast(I32),
+                in_=w1_words[e].rearrange("s p b -> p s b").bitcast(I32),
+            )
+
+        load_w1(0)
+        load_w1s()
+        make_identity(nc, ident[:])
+        def cast(copy, s, c0, c1):
+            copy(
+                out=xg[s][:, c0:c1, :].rearrange("p (c i) j -> p c j i", i=4),
+                in_=x[s][:, :, c0:c1].rearrange("p j (c i) -> p c j i", i=4),
+            )
+
+        def quantize(s):
+            nc.vector.quantize_mx(
+                out=codes[s][:].bitcast(E4M3),
+                scales=(scales[0][4 * s : P, :] if s < 2 else scales[s - 1][:]),
+                in_=xg[s][:].rearrange("p w j -> p (w j)"),
+            )
+
+        def gather(s, j0, j1):
+            entries = offsets[:, j0 // 16 : j1 // 16]
+            nc.vector.tensor_copy(gcodes[s][:, j0:j1], codes[s][:].indirect(entries))
+
+        def gather_scales(s, j0, j1):
+            entries = offsets[:, j0 // 16 : j1 // 16]
+            nc.vector.tensor_copy(gscales[s][:, j0:j1], scales[max(s - 1, 0)][:].indirect(entries))
+
+        for s in range(S):
+            if s == 0:
+                cast(nc.scalar.copy, s, 0, 256)
+                cast(nc.vector.tensor_copy, s, 256, 384)
+                cast(nc.scalar.copy, s, 384, 512)
+            else:
+                cast(nc.scalar.copy, s, 0, 192)
+                cast(nc.scalar.copy, s, 192, 384)
+                cast(nc.vector.tensor_copy, s, 384, 512)
+
+        def gather_early(s, j0, j1):
+            if s == 1:
+                gather_scales(0, j0, j1)
+                nc.scalar.dma_start(
+                    out=gscales[1][0:112, j0:j1].bitcast(I32),
+                    in_=gscales[0][4 : 4 + 112, j0:j1].bitcast(I32),
+                )
+            gather(s, j0, j1)
+            if s == 2:
+                gather_scales(s, j0, j1)
+
+        def gather_last(e):
+            gather(S - 1, C * e, C * (e + 1))
+            gather_scales(S - 1, C * e, C * (e + 1))
+
+        for s in range(S):
+            quantize(s)
+            if s < S - 1:
+                gather_early(s, 0, 384)
+        for e in range(3):
+            gather_last(e)
+        for s in range(S - 1):
+            gather_early(s, 384, 768)
+
+        def load_w2(e0, e1):
+            nc.sync.dma_start(
+                out=w2[:, e0:e1, :].bitcast(I32),
+                in_=w2_words[e0:e1].rearrange("e s p b -> p (e s) b").bitcast(I32),
+            )
+
+        load_w1(1)
+        load_w1(2)
+        for r in range(4):
+            nc.sync.dma_start(
+                out=w2s[r:P:32, :, :].bitcast(I32),
+                in_=w2_scales.rearrange("e s (b r) i -> r b (e s) i", r=4)[r].bitcast(I32),
+            )
+        load_w2(0, 6)
+        load_w1(3)
+        load_w1(4)
+        load_w1(5)
+
+        def first(e):
+            a = psum_a.tile([P, H], F32, name="a")
+            cols = slice(C * e, C * (e + 1))
+            for s in range(S):
+                nc.tensor.matmul_mx(
+                    out=a[:],
+                    lhsT=gcodes[s][:, cols].bitcast(E4M3),
+                    lhsT_scale=gscales[s][:, cols],
+                    rhs=w1[e][:, s, :].bitcast(E2M1),
+                    rhs_scale=w1s[:, S * e + s, :],
+                    start=(s == 0),
+                    stop=(s == S - 1),
+                )
+            return a
+
+        def relu(e, a):
+            r = work.tile([P, 4, P], F32, name="r", align_bytes=64)
+            src = a[:].rearrange("c (p t) -> c t p", t=4)
+            if e < 4:
+                nc.scalar.activation(r[:], src, RELU)
+            else:
+                nc.vector.tensor_scalar_max(r[:], src, 0.0)
+            return r
+
+        def turn(r):
+            t = psum_t.tile([P, 4, C], F32, name="t")
+            for d in range(4):
+                nc.tensor.transpose(t[:, d, :], r[:, d, :], ident[:])
+            return t
+
+        def square(t):
+            h = work.tile([P, C, 4], BF16, name="h", align_bytes=64)
+            nc.scalar.activation(h[:], t[:].rearrange("p t c -> p c t"), SQUARE)
+            return h
+
+        def quantize_h(h):
+            hc = work.tile([P, C], U32, name="hc", align_bytes=64)
+            hs = work.tile([P, C], U8, name="hs", align_bytes=64)
+            nc.vector.quantize_mx(out=hc[:].bitcast(E4M3), scales=hs[:], in_=h[:].rearrange("p c t -> p (c t)"))
+            return hc, hs
+
+        def second(e, hc, hs):
+            b = psum_y.tile([P, N // P, C], F32, name="b")
+            for n in range(N // P):
+                nc.tensor.matmul_mx(
+                    out=b[:, n, :],
+                    lhsT=w2[:, e, 2 * P * n : 2 * P * (n + 1)].bitcast(E2M1),
+                    lhsT_scale=w2s[:, e, P * n : P * (n + 1)],
+                    rhs=hc[:].bitcast(E4M3),
+                    rhs_scale=hs[:],
+                    start=True,
+                    stop=True,
+                )
+            return b
+
+        def collect(e, b):
+            dst = y[:, :, :, e, :]
+            src = b[:].rearrange("p n (m u) -> p n m u", m=R)
+            nc.vector.tensor_copy(dst, src)
+
+        def store(e0, e1):
+            view = out.rearrange("(n p) (m e u) -> p n m e u", p=P, m=R, e=E)
+            for n in range(N // P):
+                nc.sync.dma_start(
+                    out=view[:, n, :, e0:e1, :].rearrange("p m e u -> p m (e u)"),
+                    in_=y[:, n, :, e0:e1, :].rearrange("p m e u -> p m (e u)"),
+                )
+
+        a, r, t, q, b = {}, {}, {}, {}, {}
+        for i in range(E + 2):
+            if i < E:
+                if i >= 3:
+                    gather_last(i)
+                a[i] = first(i)
+            if 0 <= i - 1 < E:
+                t[i - 1] = turn(r[i - 1])
+            if 0 <= i - 2 < E:
+                b[i - 2] = second(i - 2, *q[i - 2])
+            if i < E:
+                r[i] = relu(i, a[i])
+            if 0 <= i - 1 < E:
+                h = square(t[i - 1])
+                q[i - 1] = quantize_h(h)
+            if 0 <= i - 2 < E:
+                collect(i - 2, b[i - 2])
+            if i - 2 == 2:
+                store(0, 3)
+            if i - 2 == 4:
+                store(3, 5)
+        store(5, 6)

@@ -7,6 +7,7 @@ K, T, E, C, H, N, R = 2048, 512, 6, 128, 512, 384, 4
 P = 128
 S = K // 512
 SLOTS = E * C
+PAIR = 2 * C
 FLOPS = 2 * SLOTS * (K * H + H * N)
 
 F32 = mybir.dt.float32
@@ -28,151 +29,164 @@ def tile_moe_eps_mlp_relu2_kernel(
     with ExitStack() as ctx:
         keep = ctx.enter_context(tc.tile_pool(name="keep", bufs=1))
         work = ctx.enter_context(tc.tile_pool(name="work", bufs=3))
-        psum_a = ctx.enter_context(tc.psum_pool(name="psum_a", bufs=4))
+        psum_a = ctx.enter_context(tc.psum_pool(name="psum_a", bufs=2))
         psum_t = ctx.enter_context(tc.psum_pool(name="psum_t", bufs=2))
-        psum_y = ctx.enter_context(tc.psum_pool(name="psum_y", bufs=2))
+        psum_y = ctx.enter_context(tc.psum_pool(name="psum_y", bufs=4))
+
+        def held(shape, dtype, name, tag=None):
+            return keep.tile(shape, dtype, name=name, tag=tag or name, align_bytes=64)
 
         offsets = keep.tile([P, SLOTS // 16], U16, name="offsets")
-        x = [keep.tile([P, 4, T], F32, name=f"x{s}") for s in range(S)]
-        xg = [keep.tile([P, T, 4], BF16, name=f"xg{s}", align_bytes=64) for s in range(S)]
-        codes = [keep.tile([P, T], U32, name=f"codes{s}", align_bytes=64) for s in range(S)]
-        scales = [keep.tile([P, T], U8, name=f"scales{i}", align_bytes=64) for i in range(3)]
-        gcodes = [keep.tile([P, SLOTS], U32, name=f"gcodes{s}", align_bytes=64) for s in range(S)]
-        gscales = [keep.tile([P, SLOTS], U8, name=f"gscales{s}", align_bytes=64) for s in range(S)]
-        w1 = [keep.tile([P, S, 2 * H], U8, name=f"w1_{e}", align_bytes=64) for e in range(E)]
-        w1s = keep.tile([P, E * S, H], U8, name="w1s", align_bytes=64)
-        w2 = keep.tile([P, E, 2 * N], U8, name="w2", align_bytes=64)
-        w2s = keep.tile([P, E, N], U8, name="w2s", align_bytes=64)
-        y = keep.tile([P, N // P, R, E, C // R], F32, name="y", align_bytes=64)
-        ident = keep.tile([P, P], F32, name="ident", align_bytes=64)
+        x0 = [held([P, 4, T // 2], F32, f"x0_{i}") for i in range(2)]
+        x = {s: held([P, 4, T], F32, f"x{s}") for s in range(1, S)}
+        xg = [held([P, T, 4], BF16, f"xg{s}") for s in range(S)]
+        codes = held([P, S * T], U32, "codes")
+        scales01 = held([P, T], U8, "scales01")
+        scales23 = held([P, 2 * T], U8, "scales23")
+        gw0 = held([P, SLOTS], U32, "gw0")
+        gb0 = held([P, SLOTS], U8, "gb0")
+        gb1 = held([P, SLOTS], U8, "gb1")
+        w1s_a = held([P, 2 * S, H], U8, "w1s_a")
+        w1s_b = held([P, (E - 2) * S, H], U8, "w1s_b")
+        w2s = held([P, E, N], U8, "w2s")
+        groups = [(0, 6)]
+        y = {e0: held([P, N // P, R, e1 - e0, C // R], F32, f"y{e0}") for e0, e1 in groups}
+        ident = held([P, P], F32, "ident")
+        w1, gw, gb = {}, {}, {}
 
-        def load_x(s, c0, c1):
-            rows = xT[512 * s : 512 * (s + 1), c0:c1].rearrange("(p j) w -> p j w", j=4)
-            nc.sync.dma_start(out=x[s][:, :, c0:c1], in_=rows)
+        def rows(s):
+            return xT[512 * s : 512 * (s + 1), :].rearrange("(p j) w -> p j w", j=4)
 
-        load_x(0, 0, 256)
+        nc.sync.dma_start(out=x0[0][:], in_=rows(0)[:, :, 0 : T // 2])
         nc.sync.dma_start(offsets[:], offs)
-        load_x(0, 256, 512)
-        load_x(1, 0, T)
-        load_x(2, 0, T)
-        load_x(3, 0, T)
+        nc.sync.dma_start(out=x0[1][:], in_=rows(0)[:, :, T // 2 : T])
+        for s in range(1, S):
+            nc.sync.dma_start(out=x[s][:], in_=rows(s))
 
-        nc.vector.memset(w1s[:].rearrange("p a i -> p (a i)").bitcast(I32), 0)
-        for plane in scales + [gscales[1]]:
-            nc.gpsimd.memset(plane[:], 0)
-        nc.gpsimd.memset(w2s[:].rearrange("p a i -> p (a i)").bitcast(I32), 0)
+        nc.vector.memset(w1s_a[:].rearrange("p a i -> p (a i)").bitcast(I32), 0)
+        for plane in (scales01, scales23, gb1):
+            nc.vector.memset(plane[:].bitcast(I32), 0)
+        nc.vector.memset(w1s_b[:].rearrange("p a i -> p (a i)").bitcast(I32), 0)
+        nc.vector.memset(w2s[:].rearrange("p a i -> p (a i)").bitcast(I32), 0)
+        make_identity(nc, ident[:])
 
-        def load_w1s():
+        def load_scales(tile, source):
             for r in range(4):
                 nc.sync.dma_start(
-                    out=w1s[r:P:32, :, :].bitcast(I32),
-                    in_=w1_scales.rearrange("e s (b r) i -> r b (e s) i", r=4)[r].bitcast(I32),
+                    out=tile[r:P:32, :, :].bitcast(I32),
+                    in_=source.rearrange("e s (b r) i -> r b (e s) i", r=4)[r].bitcast(I32),
                 )
 
-        def load_w1(e):
+        def load_w1(e, tag=None):
+            w1[e] = held([P, S, 2 * H], U8, f"w1_{e}", tag)
             nc.sync.dma_start(
                 out=w1[e][:].bitcast(I32),
                 in_=w1_words[e].rearrange("s p b -> p s b").bitcast(I32),
             )
 
+        load_scales(w1s_a, w1_scales[0:2])
         load_w1(0)
-        load_w1s()
-        make_identity(nc, ident[:])
-        def cast(copy, s, c0, c1):
+        load_w1(1)
+        load_scales(w1s_b, w1_scales[2:E])
+
+        def cast(copy, s, source, c0, c1, base=0):
             copy(
                 out=xg[s][:, c0:c1, :].rearrange("p (c i) j -> p c j i", i=4),
-                in_=x[s][:, :, c0:c1].rearrange("p j (c i) -> p c j i", i=4),
+                in_=source[:, :, c0 - base : c1 - base].rearrange("p j (c i) -> p c j i", i=4),
             )
 
         def quantize(s):
+            plane = scales01[4 * s : P, :] if s < 2 else scales23[:, T * (s - 2) : T * (s - 1)]
             nc.vector.quantize_mx(
-                out=codes[s][:].bitcast(E4M3),
-                scales=(scales[0][4 * s : P, :] if s < 2 else scales[s - 1][:]),
+                out=codes[:, T * s : T * (s + 1)].bitcast(E4M3),
+                scales=plane,
                 in_=xg[s][:].rearrange("p w j -> p (w j)"),
             )
 
-        def gather(s, j0, j1):
-            entries = offsets[:, j0 // 16 : j1 // 16]
-            nc.vector.tensor_copy(gcodes[s][:, j0:j1], codes[s][:].indirect(entries))
+        def entries(j0, j1):
+            return offsets[:, j0 // 16 : j1 // 16]
 
-        def gather_scales(s, j0, j1):
-            entries = offsets[:, j0 // 16 : j1 // 16]
-            nc.vector.tensor_copy(gscales[s][:, j0:j1], scales[max(s - 1, 0)][:].indirect(entries))
+        def gather_words(g, s, j0, j1, whole):
+            window = codes[:, T * s : (S * T if whole else T * (s + 1))]
+            dst = gw[g][:, PAIR * (s - 1) + j0 : PAIR * (s - 1) + j1]
+            nc.vector.tensor_copy(dst, window.indirect(entries(PAIR * g + j0, PAIR * g + j1)))
 
-        for s in range(S):
-            if s == 0:
-                cast(nc.scalar.copy, s, 0, 256)
-                cast(nc.vector.tensor_copy, s, 256, 384)
-                cast(nc.scalar.copy, s, 384, 512)
-            else:
-                cast(nc.scalar.copy, s, 0, 192)
-                cast(nc.scalar.copy, s, 192, 384)
-                cast(nc.vector.tensor_copy, s, 384, 512)
+        def gather_bytes(g, s, j0, j1, whole):
+            window = scales23[:, T * (s - 2) : (2 * T if whole else T * (s - 1))]
+            dst = gb[g][:, PAIR * (s - 2) + j0 : PAIR * (s - 2) + j1]
+            nc.vector.tensor_copy(dst, window.indirect(entries(PAIR * g + j0, PAIR * g + j1)))
 
-        def gather_early(s, j0, j1):
-            if s == 1:
-                gather_scales(0, j0, j1)
-                nc.scalar.dma_start(
-                    out=gscales[1][0:112, j0:j1].bitcast(I32),
-                    in_=gscales[0][4 : 4 + 112, j0:j1].bitcast(I32),
-                )
-            gather(s, j0, j1)
-            if s == 2:
-                gather_scales(s, j0, j1)
+        gw[0] = held([P, 3 * PAIR], U32, "gw_0")
+        gb[0] = held([P, 2 * PAIR], U8, "gb_0")
 
-        def gather_last(e):
-            gather(S - 1, C * e, C * (e + 1))
-            gather_scales(S - 1, C * e, C * (e + 1))
-
-        for s in range(S):
+        cast(nc.scalar.copy, 0, x0[0], 0, 256)
+        cast(nc.vector.tensor_copy, 0, x0[1], 256, 512, 256)
+        quantize(0)
+        for j in (0, 384):
+            nc.vector.tensor_copy(gw0[:, j : j + 384], codes[:, 0:T].indirect(entries(j, j + 384)))
+        for s in range(1, S):
+            split = (320, 448, 320)[s - 1]
+            cast(nc.scalar.copy, s, x[s], 0, split)
+            cast(nc.vector.tensor_copy, s, x[s], split, T)
             quantize(s)
-            if s < S - 1:
-                gather_early(s, 0, 384)
-        for e in range(3):
-            gather_last(e)
-        for s in range(S - 1):
-            gather_early(s, 384, 768)
+            if s == 1:
+                for j in (0, 384):
+                    nc.vector.tensor_copy(gb0[:, j : j + 384], scales01[:].indirect(entries(j, j + 384)))
+        nc.scalar.dma_start(out=gb1[0:112, :].bitcast(I32), in_=gb0[4 : 4 + 112, :].bitcast(I32))
+        gather_words(0, 1, 0, PAIR, False)
+        gather_words(0, 2, 0, PAIR, False)
+        gather_bytes(0, 2, 0, PAIR, False)
+        for j in (0, C):
+            gather_words(0, 3, j, j + C, False)
+            gather_bytes(0, 3, j, j + C, False)
 
-        def load_w2(e0, e1):
-            nc.sync.dma_start(
-                out=w2[:, e0:e1, :].bitcast(I32),
-                in_=w2_words[e0:e1].rearrange("e s p b -> p (e s) b").bitcast(I32),
-            )
+        load_w1(2, "x0_0")
+        load_w1(3, "x0_1")
+        load_w1(4, "x1")
+        load_w1(5, "x2")
+        w2 = held([P, E, 2 * N], U8, "w2", "x3")
+        load_scales(w2s, w2_scales)
+        nc.sync.dma_start(
+            out=w2[:].bitcast(I32),
+            in_=w2_words.rearrange("e s p b -> p (e s) b").bitcast(I32),
+        )
 
-        load_w1(1)
-        load_w1(2)
-        for r in range(4):
-            nc.sync.dma_start(
-                out=w2s[r:P:32, :, :].bitcast(I32),
-                in_=w2_scales.rearrange("e s (b r) i -> r b (e s) i", r=4)[r].bitcast(I32),
-            )
-        load_w2(0, 6)
-        load_w1(3)
-        load_w1(4)
-        load_w1(5)
+        def pair_words(g, tag=None):
+            gw[g] = held([P, 3 * PAIR], U32, f"gw_{g}", tag)
+            for s in range(1, S):
+                gather_words(g, s, 0, PAIR, True)
+
+        def pair_bytes(g, tag=None):
+            gb[g] = held([P, 2 * PAIR], U8, f"gb_{g}", tag)
+            for s in range(2, S):
+                gather_bytes(g, s, 0, PAIR, True)
 
         def first(e):
             a = psum_a.tile([P, H], F32, name="a")
-            cols = slice(C * e, C * (e + 1))
+            g, j = divmod(C * e, PAIR)
             for s in range(S):
+                if s == 0:
+                    words = gw0[:, C * e : C * (e + 1)]
+                else:
+                    words = gw[g][:, PAIR * (s - 1) + j : PAIR * (s - 1) + j + C]
+                if s < 2:
+                    plane = (gb0, gb1)[s][:, C * e : C * (e + 1)]
+                else:
+                    plane = gb[g][:, PAIR * (s - 2) + j : PAIR * (s - 2) + j + C]
                 nc.tensor.matmul_mx(
                     out=a[:],
-                    lhsT=gcodes[s][:, cols].bitcast(E4M3),
-                    lhsT_scale=gscales[s][:, cols],
+                    lhsT=words.bitcast(E4M3),
+                    lhsT_scale=plane,
                     rhs=w1[e][:, s, :].bitcast(E2M1),
-                    rhs_scale=w1s[:, S * e + s, :],
+                    rhs_scale=w1s_a[:, S * e + s, :] if e < 2 else w1s_b[:, S * (e - 2) + s, :],
                     start=(s == 0),
                     stop=(s == S - 1),
                 )
             return a
 
-        def relu(e, a):
+        def relu(a):
             r = work.tile([P, 4, P], F32, name="r", align_bytes=64)
-            src = a[:].rearrange("c (p t) -> c t p", t=4)
-            if e < 4:
-                nc.scalar.activation(r[:], src, RELU)
-            else:
-                nc.vector.tensor_scalar_max(r[:], src, 0.0)
+            nc.scalar.activation(r[:], a[:].rearrange("c (p t) -> c t p", t=4), RELU)
             return r
 
         def turn(r):
@@ -181,14 +195,14 @@ def tile_moe_eps_mlp_relu2_kernel(
                 nc.tensor.transpose(t[:, d, :], r[:, d, :], ident[:])
             return t
 
-        def square(t):
-            h = work.tile([P, C, 4], BF16, name="h", align_bytes=64)
+        def square(e, t):
+            h = held([P, C, 4], BF16, f"h{e}")
             nc.scalar.activation(h[:], t[:].rearrange("p t c -> p c t"), SQUARE)
             return h
 
-        def quantize_h(h):
-            hc = work.tile([P, C], U32, name="hc", align_bytes=64)
-            hs = work.tile([P, C], U8, name="hs", align_bytes=64)
+        def quantize_h(e, h):
+            hc = held([P, C], U32, f"hc{e}")
+            hs = held([P, C], U8, f"hs{e}")
             nc.vector.quantize_mx(out=hc[:].bitcast(E4M3), scales=hs[:], in_=h[:].rearrange("p c t -> p (c t)"))
             return hc, hs
 
@@ -207,37 +221,32 @@ def tile_moe_eps_mlp_relu2_kernel(
             return b
 
         def collect(e, b):
-            dst = y[:, :, :, e, :]
-            src = b[:].rearrange("p n (m u) -> p n m u", m=R)
-            nc.vector.tensor_copy(dst, src)
+            copy = nc.scalar.copy if e % 2 == 1 else nc.vector.tensor_copy
+            e0 = max(g0 for g0, g1 in groups if g0 <= e)
+            copy(y[e0][:, :, :, e - e0, :], b[:].rearrange("p n (m u) -> p n m u", m=R))
 
         def store(e0, e1):
             view = out.rearrange("(n p) (m e u) -> p n m e u", p=P, m=R, e=E)
             for n in range(N // P):
                 nc.sync.dma_start(
                     out=view[:, n, :, e0:e1, :].rearrange("p m e u -> p m (e u)"),
-                    in_=y[:, n, :, e0:e1, :].rearrange("p m e u -> p m (e u)"),
+                    in_=y[e0][:, n, :, :, :].rearrange("p m e u -> p m (e u)"),
                 )
 
-        a, r, t, q, b = {}, {}, {}, {}, {}
-        for i in range(E + 2):
+        for g in (1, 2):
+            pair_words(g)
+            pair_bytes(g)
+        a, r, q = {}, {}, {}
+        for i in range(E + 1):
             if i < E:
-                if i >= 3:
-                    gather_last(i)
                 a[i] = first(i)
-            if 0 <= i - 1 < E:
-                t[i - 1] = turn(r[i - 1])
-            if 0 <= i - 2 < E:
-                b[i - 2] = second(i - 2, *q[i - 2])
+            if i > 0:
+                t = turn(r[i - 1])
             if i < E:
-                r[i] = relu(i, a[i])
-            if 0 <= i - 1 < E:
-                h = square(t[i - 1])
-                q[i - 1] = quantize_h(h)
-            if 0 <= i - 2 < E:
-                collect(i - 2, b[i - 2])
-            if i - 2 == 2:
-                store(0, 3)
-            if i - 2 == 4:
-                store(3, 5)
-        store(5, 6)
+                r[i] = relu(a[i])
+            if i > 0:
+                q[i - 1] = quantize_h(i - 1, square(i - 1, t))
+        for e0, e1 in groups:
+            for e in range(e0, e1):
+                collect(e, second(e, *q[e]))
+            store(e0, e1)

@@ -28,7 +28,7 @@ def tile_moe_eps_mlp_relu2_kernel(
     nc = tc.nc
     with ExitStack() as ctx:
         keep = ctx.enter_context(tc.tile_pool(name="keep", bufs=1))
-        work = ctx.enter_context(tc.tile_pool(name="work", bufs=3))
+        work = ctx.enter_context(tc.tile_pool(name="work", bufs=4))
         psum_a = ctx.enter_context(tc.psum_pool(name="psum_a", bufs=2))
         psum_t = ctx.enter_context(tc.psum_pool(name="psum_t", bufs=2))
         psum_y = ctx.enter_context(tc.psum_pool(name="psum_y", bufs=4))
@@ -46,11 +46,10 @@ def tile_moe_eps_mlp_relu2_kernel(
         gw0 = held([P, SLOTS], U32, "gw0")
         gb0 = held([P, SLOTS], U8, "gb0")
         gb1 = held([P, SLOTS], U8, "gb1")
-        w1s_a = held([P, 2 * S, H], U8, "w1s_a")
-        w1s_b = held([P, (E - 2) * S, H], U8, "w1s_b")
+        w1s_a = held([P, 3 * S, H], U8, "w1s_a")
+        w1s_b = held([P, 3 * S, H], U8, "w1s_b")
         w2s = held([P, E, N], U8, "w2s")
-        groups = [(0, 6)]
-        y = {e0: held([P, N // P, R, e1 - e0, C // R], F32, f"y{e0}") for e0, e1 in groups}
+        y = [held([P, R, E, C // R], F32, f"y{n}") for n in range(N // P)]
         ident = held([P, P], F32, "ident")
         w1, gw, gb = {}, {}, {}
 
@@ -66,8 +65,8 @@ def tile_moe_eps_mlp_relu2_kernel(
         nc.vector.memset(w1s_a[:].rearrange("p a i -> p (a i)").bitcast(I32), 0)
         for plane in (scales01, scales23, gb1):
             nc.vector.memset(plane[:].bitcast(I32), 0)
-        nc.vector.memset(w1s_b[:].rearrange("p a i -> p (a i)").bitcast(I32), 0)
-        nc.vector.memset(w2s[:].rearrange("p a i -> p (a i)").bitcast(I32), 0)
+        nc.gpsimd.memset(w1s_b[:].rearrange("p a i -> p (a i)").bitcast(I32), 0)
+        nc.gpsimd.memset(w2s[:].rearrange("p a i -> p (a i)").bitcast(I32), 0)
         make_identity(nc, ident[:])
 
         def load_scales(tile, source):
@@ -78,16 +77,25 @@ def tile_moe_eps_mlp_relu2_kernel(
                 )
 
         def load_w1(e, tag=None):
-            w1[e] = held([P, S, 2 * H], U8, f"w1_{e}", tag)
+            words = held([P, S, 2 * H], U8, f"w1_{e}", tag)
             nc.sync.dma_start(
-                out=w1[e][:].bitcast(I32),
+                out=words[:].bitcast(I32),
                 in_=w1_words[e].rearrange("s p b -> p s b").bitcast(I32),
             )
+            for s in range(S):
+                w1[e, s] = words[:, s, :]
 
-        load_scales(w1s_a, w1_scales[0:2])
-        load_w1(0)
-        load_w1(1)
-        load_scales(w1s_b, w1_scales[2:E])
+        load_scales(w1s_a, w1_scales[0:3])
+        for s in range(S):
+            both = held([P, 2, 2 * H], U8, f"w1_pass{s}")
+            nc.sync.dma_start(
+                out=both[:].bitcast(I32),
+                in_=w1_words[0:2, s].rearrange("e p b -> p e b").bitcast(I32),
+            )
+            for e in range(2):
+                w1[e, s] = both[:, e, :]
+        load_w1(2)
+        load_scales(w1s_b, w1_scales[3:E])
 
         def cast(copy, s, source, c0, c1, base=0):
             copy(
@@ -95,12 +103,12 @@ def tile_moe_eps_mlp_relu2_kernel(
                 in_=source[:, :, c0 - base : c1 - base].rearrange("p j (c i) -> p c j i", i=4),
             )
 
-        def quantize(s):
-            plane = scales01[4 * s : P, :] if s < 2 else scales23[:, T * (s - 2) : T * (s - 1)]
+        def quantize(s, c0=0, c1=T):
+            plane = scales01[4 * s : P, c0:c1] if s < 2 else scales23[:, T * (s - 2) + c0 : T * (s - 2) + c1]
             nc.vector.quantize_mx(
-                out=codes[:, T * s : T * (s + 1)].bitcast(E4M3),
+                out=codes[:, T * s + c0 : T * s + c1].bitcast(E4M3),
                 scales=plane,
-                in_=xg[s][:].rearrange("p w j -> p (w j)"),
+                in_=xg[s][:, c0:c1, :].rearrange("p w j -> p (w j)"),
             )
 
         def entries(j0, j1):
@@ -116,18 +124,23 @@ def tile_moe_eps_mlp_relu2_kernel(
             dst = gb[g][:, PAIR * (s - 2) + j0 : PAIR * (s - 2) + j1]
             nc.vector.tensor_copy(dst, window.indirect(entries(PAIR * g + j0, PAIR * g + j1)))
 
-        gw[0] = held([P, 3 * PAIR], U32, "gw_0")
-        gb[0] = held([P, 2 * PAIR], U8, "gb_0")
+        for g in range(E // 2):
+            gw[g] = held([P, 3 * PAIR], U32, f"gw_{g}")
+            gb[g] = held([P, 2 * PAIR], U8, f"gb_{g}")
 
-        cast(nc.scalar.copy, 0, x0[0], 0, 256)
-        cast(nc.vector.tensor_copy, 0, x0[1], 256, 512, 256)
-        quantize(0)
+        cast(nc.scalar.copy, 0, x0[0], 0, 96)
+        cast(nc.vector.tensor_copy, 0, x0[0], 96, 256)
+        cast(nc.scalar.copy, 0, x0[1], 256, 352, 256)
+        quantize(0, 0, 256)
+        cast(nc.vector.tensor_copy, 0, x0[1], 352, 512, 256)
+        quantize(0, 256, 512)
         for j in (0, 384):
             nc.vector.tensor_copy(gw0[:, j : j + 384], codes[:, 0:T].indirect(entries(j, j + 384)))
         for s in range(1, S):
-            split = (320, 448, 320)[s - 1]
+            split = (320, 512, 512)[s - 1]
             cast(nc.scalar.copy, s, x[s], 0, split)
-            cast(nc.vector.tensor_copy, s, x[s], split, T)
+            if split < T:
+                cast(nc.vector.tensor_copy, s, x[s], split, T)
             quantize(s)
             if s == 1:
                 for j in (0, 384):
@@ -140,31 +153,25 @@ def tile_moe_eps_mlp_relu2_kernel(
             gather_words(0, 3, j, j + C, False)
             gather_bytes(0, 3, j, j + C, False)
 
-        load_w1(2, "x0_0")
-        load_w1(3, "x0_1")
-        load_w1(4, "x1")
-        load_w1(5, "x2")
+        load_w1(3, "x0_0")
+        load_w1(4, "x0_1")
+        load_w1(5, "x1")
         w2 = held([P, E, 2 * N], U8, "w2", "x3")
         load_scales(w2s, w2_scales)
-        nc.sync.dma_start(
-            out=w2[:].bitcast(I32),
-            in_=w2_words.rearrange("e s p b -> p (e s) b").bitcast(I32),
-        )
+        for e0 in (0, 3):
+            nc.sync.dma_start(
+                out=w2[:, e0 : e0 + 3, :].bitcast(I32),
+                in_=w2_words[e0 : e0 + 3].rearrange("e s p b -> p (e s) b").bitcast(I32),
+            )
 
-        def pair_words(g, tag=None):
-            gw[g] = held([P, 3 * PAIR], U32, f"gw_{g}", tag)
-            for s in range(1, S):
-                gather_words(g, s, 0, PAIR, True)
-
-        def pair_bytes(g, tag=None):
-            gb[g] = held([P, 2 * PAIR], U8, f"gb_{g}", tag)
+        def gather_late(g, j0, j1):
             for s in range(2, S):
-                gather_bytes(g, s, 0, PAIR, True)
+                gather_words(g, s, j0, j1, True)
+                gather_bytes(g, s, j0, j1, True)
 
-        def first(e):
-            a = psum_a.tile([P, H], F32, name="a")
+        def first(e, a, passes):
             g, j = divmod(C * e, PAIR)
-            for s in range(S):
+            for s in passes:
                 if s == 0:
                     words = gw0[:, C * e : C * (e + 1)]
                 else:
@@ -177,12 +184,11 @@ def tile_moe_eps_mlp_relu2_kernel(
                     out=a[:],
                     lhsT=words.bitcast(E4M3),
                     lhsT_scale=plane,
-                    rhs=w1[e][:, s, :].bitcast(E2M1),
-                    rhs_scale=w1s_a[:, S * e + s, :] if e < 2 else w1s_b[:, S * (e - 2) + s, :],
+                    rhs=w1[e, s].bitcast(E2M1),
+                    rhs_scale=w1s_a[:, S * e + s, :] if e < 3 else w1s_b[:, S * (e - 3) + s, :],
                     start=(s == 0),
                     stop=(s == S - 1),
                 )
-            return a
 
         def relu(a):
             r = work.tile([P, 4, P], F32, name="r", align_bytes=64)
@@ -206,47 +212,45 @@ def tile_moe_eps_mlp_relu2_kernel(
             nc.vector.quantize_mx(out=hc[:].bitcast(E4M3), scales=hs[:], in_=h[:].rearrange("p c t -> p (c t)"))
             return hc, hs
 
-        def second(e, hc, hs):
-            b = psum_y.tile([P, N // P, C], F32, name="b")
+        def second(e, n, b):
+            hc, hs = q[e]
+            nc.tensor.matmul_mx(
+                out=b,
+                lhsT=w2[:, e, 2 * P * n : 2 * P * (n + 1)].bitcast(E2M1),
+                lhsT_scale=w2s[:, e, P * n : P * (n + 1)],
+                rhs=hc[:].bitcast(E4M3),
+                rhs_scale=hs[:],
+                start=True,
+                stop=True,
+            )
+
+        def results(e0):
+            banks = [psum_y.tile([P, 3, C], F32, name="b") for n in range(N // P)]
+            for e in range(e0, e0 + 3):
+                for n in range(N // P):
+                    second(e, n, banks[n][:, e - e0, :])
             for n in range(N // P):
-                nc.tensor.matmul_mx(
-                    out=b[:, n, :],
-                    lhsT=w2[:, e, 2 * P * n : 2 * P * (n + 1)].bitcast(E2M1),
-                    lhsT_scale=w2s[:, e, P * n : P * (n + 1)],
-                    rhs=hc[:].bitcast(E4M3),
-                    rhs_scale=hs[:],
-                    start=True,
-                    stop=True,
-                )
-            return b
+                copy = nc.scalar.copy if n == 1 else nc.vector.tensor_copy
+                copy(y[n][:, :, e0 : e0 + 3, :], banks[n][:].rearrange("p e (m u) -> p m e u", m=R))
 
-        def collect(e, b):
-            copy = nc.scalar.copy if e % 2 == 1 else nc.vector.tensor_copy
-            e0 = max(g0 for g0, g1 in groups if g0 <= e)
-            copy(y[e0][:, :, :, e - e0, :], b[:].rearrange("p n (m u) -> p n m u", m=R))
-
-        def store(e0, e1):
-            view = out.rearrange("(n p) (m e u) -> p n m e u", p=P, m=R, e=E)
-            for n in range(N // P):
-                nc.sync.dma_start(
-                    out=view[:, n, :, e0:e1, :].rearrange("p m e u -> p m (e u)"),
-                    in_=y[e0][:, n, :, :, :].rearrange("p m e u -> p m (e u)"),
-                )
-
-        for g in (1, 2):
-            pair_words(g)
-            pair_bytes(g)
-        a, r, q = {}, {}, {}
-        for i in range(E + 1):
-            if i < E:
-                a[i] = first(i)
-            if i > 0:
-                t = turn(r[i - 1])
-            if i < E:
-                r[i] = relu(a[i])
-            if i > 0:
-                q[i - 1] = quantize_h(i - 1, square(i - 1, t))
-        for e0, e1 in groups:
-            for e in range(e0, e1):
-                collect(e, second(e, *q[e]))
-            store(e0, e1)
+        gather_words(1, 1, 0, PAIR, True)
+        gather_late(1, 0, C)
+        gather_late(1, C, PAIR)
+        gather_words(2, 1, 0, PAIR, True)
+        gather_late(2, 0, C)
+        gather_late(2, C, PAIR)
+        a, q = {}, {}
+        for e in range(2):
+            a[e] = psum_a.tile([P, H], F32, name="a")
+        for s in range(S):
+            first(0, a[0], [s])
+            first(1, a[1], [s])
+        for e in range(E):
+            q[e] = quantize_h(e, square(e, turn(relu(a[e]))))
+            if e + 2 < E:
+                a[e + 2] = psum_a.tile([P, H], F32, name="a")
+                first(e + 2, a[e + 2], range(S))
+        results(0)
+        results(3)
+        for n in range(N // P):
+            nc.sync.dma_start(out=out[P * n : P * (n + 1), :], in_=y[n][:].rearrange("p m e u -> p (m e u)"))

@@ -8,6 +8,7 @@ P = 128
 S = K // 512
 SLOTS = E * C
 PAIR = 2 * C
+ORDER = (0, 2, 3, 1)
 FLOPS = 2 * SLOTS * (K * H + H * N)
 
 F32 = mybir.dt.float32
@@ -37,8 +38,7 @@ def tile_moe_eps_mlp_relu2_kernel(
             return keep.tile(shape, dtype, name=name, tag=tag or name, align_bytes=64)
 
         offsets = keep.tile([P, SLOTS // 16], U16, name="offsets")
-        x0 = [held([P, 4, T // 2], F32, f"x0_{i}") for i in range(2)]
-        x = {s: held([P, 4, T], F32, f"x{s}") for s in range(1, S)}
+        x = [held([P, 4, T], F32, f"x{s}") for s in range(S)]
         xg = [held([P, T, 4], BF16, f"xg{s}") for s in range(S)]
         codes = held([P, S * T], U32, "codes")
         scales01 = held([P, T], U8, "scales01")
@@ -56,9 +56,8 @@ def tile_moe_eps_mlp_relu2_kernel(
         def rows(s):
             return xT[512 * s : 512 * (s + 1), :].rearrange("(p j) w -> p j w", j=4)
 
-        nc.sync.dma_start(out=x0[0][:], in_=rows(0)[:, :, 0 : T // 2])
+        nc.sync.dma_start(out=x[0][:], in_=rows(0))
         nc.sync.dma_start(offsets[:], offs)
-        nc.sync.dma_start(out=x0[1][:], in_=rows(0)[:, :, T // 2 : T])
         for s in range(1, S):
             nc.sync.dma_start(out=x[s][:], in_=rows(s))
 
@@ -66,7 +65,7 @@ def tile_moe_eps_mlp_relu2_kernel(
         for plane in (scales01, scales23, gb1):
             nc.vector.memset(plane[:].bitcast(I32), 0)
         nc.gpsimd.memset(w1s_b[:].rearrange("p a i -> p (a i)").bitcast(I32), 0)
-        nc.gpsimd.memset(w2s[:].rearrange("p a i -> p (a i)").bitcast(I32), 0)
+        nc.vector.memset(w2s[:].rearrange("p a i -> p (a i)").bitcast(I32), 0)
         make_identity(nc, ident[:])
 
         def load_scales(tile, source):
@@ -76,17 +75,16 @@ def tile_moe_eps_mlp_relu2_kernel(
                     in_=source.rearrange("e s (b r) i -> r b (e s) i", r=4)[r].bitcast(I32),
                 )
 
-        def load_w1(e, tag=None):
-            words = held([P, S, 2 * H], U8, f"w1_{e}", tag)
+        def load_w1(e, tag=None, s0=0, s1=S):
+            words = held([P, s1 - s0, 2 * H], U8, f"w1_{e}_{s0}", tag)
             nc.sync.dma_start(
                 out=words[:].bitcast(I32),
-                in_=w1_words[e].rearrange("s p b -> p s b").bitcast(I32),
+                in_=w1_words[e, s0:s1].rearrange("s p b -> p s b").bitcast(I32),
             )
-            for s in range(S):
-                w1[e, s] = words[:, s, :]
+            for s in range(s0, s1):
+                w1[e, s] = words[:, s - s0, :]
 
-        load_scales(w1s_a, w1_scales[0:3])
-        for s in range(S):
+        def load_first_pair(s):
             both = held([P, 2, 2 * H], U8, f"w1_pass{s}")
             nc.sync.dma_start(
                 out=both[:].bitcast(I32),
@@ -94,21 +92,26 @@ def tile_moe_eps_mlp_relu2_kernel(
             )
             for e in range(2):
                 w1[e, s] = both[:, e, :]
+
+        load_scales(w1s_a, w1_scales[0:3])
+        for e in range(2):
+            load_w1(e, None, 0, S - 1)
+        load_first_pair(S - 1)
         load_w1(2)
         load_scales(w1s_b, w1_scales[3:E])
 
-        def cast(copy, s, source, c0, c1, base=0):
+        def cast(copy, s, source, c0, c1):
             copy(
                 out=xg[s][:, c0:c1, :].rearrange("p (c i) j -> p c j i", i=4),
-                in_=source[:, :, c0 - base : c1 - base].rearrange("p j (c i) -> p c j i", i=4),
+                in_=source[:, :, c0:c1].rearrange("p j (c i) -> p c j i", i=4),
             )
 
-        def quantize(s, c0=0, c1=T):
-            plane = scales01[4 * s : P, c0:c1] if s < 2 else scales23[:, T * (s - 2) + c0 : T * (s - 2) + c1]
+        def quantize(s):
+            plane = scales01[4 * s : P, :] if s < 2 else scales23[:, T * (s - 2) : T * (s - 1)]
             nc.vector.quantize_mx(
-                out=codes[:, T * s + c0 : T * s + c1].bitcast(E4M3),
+                out=codes[:, T * s : T * (s + 1)].bitcast(E4M3),
                 scales=plane,
-                in_=xg[s][:, c0:c1, :].rearrange("p w j -> p (w j)"),
+                in_=xg[s][:].rearrange("p w j -> p (w j)"),
             )
 
         def entries(j0, j1):
@@ -128,16 +131,12 @@ def tile_moe_eps_mlp_relu2_kernel(
             gw[g] = held([P, 3 * PAIR], U32, f"gw_{g}")
             gb[g] = held([P, 2 * PAIR], U8, f"gb_{g}")
 
-        cast(nc.scalar.copy, 0, x0[0], 0, 96)
-        cast(nc.vector.tensor_copy, 0, x0[0], 96, 256)
-        cast(nc.scalar.copy, 0, x0[1], 256, 352, 256)
-        quantize(0, 0, 256)
-        cast(nc.vector.tensor_copy, 0, x0[1], 352, 512, 256)
-        quantize(0, 256, 512)
-        for j in (0, 384):
-            nc.vector.tensor_copy(gw0[:, j : j + 384], codes[:, 0:T].indirect(entries(j, j + 384)))
+        cast(nc.scalar.copy, 0, x[0], 0, 192)
+        cast(nc.vector.tensor_copy, 0, x[0], 192, T)
+        quantize(0)
+        nc.vector.tensor_copy(gw0[:, 0:384], codes[:, 0:T].indirect(entries(0, 384)))
         for s in range(1, S):
-            split = (320, 512, 512)[s - 1]
+            split = (256, 512, 384)[s - 1]
             cast(nc.scalar.copy, s, x[s], 0, split)
             if split < T:
                 cast(nc.vector.tensor_copy, s, x[s], split, T)
@@ -153,9 +152,10 @@ def tile_moe_eps_mlp_relu2_kernel(
             gather_words(0, 3, j, j + C, False)
             gather_bytes(0, 3, j, j + C, False)
 
-        load_w1(3, "x0_0")
-        load_w1(4, "x0_1")
-        load_w1(5, "x1")
+        load_w1(3, "x0")
+        load_w1(4, "xg0")
+        load_w1(5, "x1", 0, S - 1)
+        load_w1(5, "xg1", S - 1, S)
         w2 = held([P, E, 2 * N], U8, "w2", "x3")
         load_scales(w2s, w2_scales)
         for e0 in (0, 3):
@@ -187,12 +187,14 @@ def tile_moe_eps_mlp_relu2_kernel(
                     rhs=w1[e, s].bitcast(E2M1),
                     rhs_scale=w1s_a[:, S * e + s, :] if e < 3 else w1s_b[:, S * (e - 3) + s, :],
                     start=(s == 0),
-                    stop=(s == S - 1),
+                    stop=(s == (ORDER[-1] if e < 2 else S - 1)),
                 )
 
-        def relu(a):
+        def relu(e, a):
             r = work.tile([P, 4, P], F32, name="r", align_bytes=64)
-            nc.scalar.activation(r[:], a[:].rearrange("c (p t) -> c t p", t=4), RELU)
+            step = 2 if e == E - 1 else 4
+            for d in range(0, 4, step):
+                nc.scalar.activation(r[:, d : d + step, :], a[:].rearrange("c (p t) -> c t p", t=4)[:, d : d + step, :], RELU)
             return r
 
         def turn(r):
@@ -235,6 +237,7 @@ def tile_moe_eps_mlp_relu2_kernel(
 
         gather_words(1, 1, 0, PAIR, True)
         gather_late(1, 0, C)
+        nc.vector.tensor_copy(gw0[:, 384:SLOTS], codes[:].indirect(entries(384, SLOTS)))
         gather_late(1, C, PAIR)
         gather_words(2, 1, 0, PAIR, True)
         gather_late(2, 0, C)
@@ -242,11 +245,11 @@ def tile_moe_eps_mlp_relu2_kernel(
         a, q = {}, {}
         for e in range(2):
             a[e] = psum_a.tile([P, H], F32, name="a")
-        for s in range(S):
-            first(0, a[0], [s])
-            first(1, a[1], [s])
+        for passes in (ORDER[:2], ORDER[2:3], ORDER[3:]):
+            first(0, a[0], passes)
+            first(1, a[1], passes)
         for e in range(E):
-            q[e] = quantize_h(e, square(e, turn(relu(a[e]))))
+            q[e] = quantize_h(e, square(e, turn(relu(e, a[e]))))
             if e + 2 < E:
                 a[e + 2] = psum_a.tile([P, H], F32, name="a")
                 first(e + 2, a[e + 2], range(S))

@@ -68,12 +68,15 @@ def tile_moe_eps_mlp_relu2_kernel(
         nc.vector.memset(w2s[:].rearrange("p a i -> p (a i)").bitcast(I32), 0)
         make_identity(nc, ident[:])
 
-        def load_scales(tile, source):
-            for r in range(4):
-                nc.sync.dma_start(
-                    out=tile[r:P:32, :, :].bitcast(I32),
-                    in_=source.rearrange("e s (b r) i -> r b (e s) i", r=4)[r].bitcast(I32),
-                )
+        def load_scales(tile, source, parts=1):
+            planes = source.rearrange("e s (b r) i -> r b (e s) i", r=4)
+            width = tile.shape[1] // parts
+            for a in range(0, tile.shape[1], width):
+                for r in range(4):
+                    nc.sync.dma_start(
+                        out=tile[r:P:32, a : a + width, :].bitcast(I32),
+                        in_=planes[r][:, a : a + width, :].bitcast(I32),
+                    )
 
         def load_w1(e, tag=None, s0=0, s1=S):
             words = held([P, s1 - s0, 2 * H], U8, f"w1_{e}_{s0}", tag)
@@ -93,12 +96,12 @@ def tile_moe_eps_mlp_relu2_kernel(
             for e in range(2):
                 w1[e, s] = both[:, e, :]
 
-        load_scales(w1s_a, w1_scales[0:3])
+        load_scales(w1s_a, w1_scales[0:3], 2)
         for e in range(2):
             load_w1(e, None, 0, S - 1)
         load_first_pair(S - 1)
         load_w1(2)
-        load_scales(w1s_b, w1_scales[3:E])
+        load_scales(w1s_b, w1_scales[3:E], 2)
 
         def cast(copy, s, source, c0, c1):
             copy(

@@ -7,8 +7,6 @@ K, T, E, C, H, N, R = 2048, 512, 6, 128, 512, 384, 4
 P = 128
 S = K // 512
 SLOTS = E * C
-PAIR = 2 * C
-ORDER = (0, 2, 3, 1)
 FLOPS = 2 * SLOTS * (K * H + H * N)
 
 F32 = mybir.dt.float32
@@ -29,10 +27,9 @@ def tile_moe_eps_mlp_relu2_kernel(
     nc = tc.nc
     with ExitStack() as ctx:
         keep = ctx.enter_context(tc.tile_pool(name="keep", bufs=1))
-        work = ctx.enter_context(tc.tile_pool(name="work", bufs=4))
-        psum_a = ctx.enter_context(tc.psum_pool(name="psum_a", bufs=2))
+        psum_a = ctx.enter_context(tc.psum_pool(name="psum_a", bufs=3))
         psum_t = ctx.enter_context(tc.psum_pool(name="psum_t", bufs=2))
-        psum_y = ctx.enter_context(tc.psum_pool(name="psum_y", bufs=4))
+        psum_y = ctx.enter_context(tc.psum_pool(name="psum_y", bufs=3))
 
         def held(shape, dtype, name, tag=None):
             return keep.tile(shape, dtype, name=name, tag=tag or name, align_bytes=64)
@@ -41,13 +38,12 @@ def tile_moe_eps_mlp_relu2_kernel(
         x = [held([P, 4, T], F32, f"x{s}") for s in range(S)]
         xg = [held([P, T, 4], BF16, f"xg{s}") for s in range(S)]
         codes = held([P, S * T], U32, "codes")
-        scales01 = held([P, T], U8, "scales01")
+        packed = held([P, T], U8, "packed")
         scales23 = held([P, 2 * T], U8, "scales23")
-        gw0 = held([P, SLOTS], U32, "gw0")
-        gb0 = held([P, SLOTS], U8, "gb0")
-        gb1 = held([P, SLOTS], U8, "gb1")
-        w1s_a = held([P, 3 * S, H], U8, "w1s_a")
-        w1s_b = held([P, 3 * S, H], U8, "w1s_b")
+        planes = [held([P, SLOTS], U8, f"plane{s}") for s in range(2)]
+        runs = ((0, 1), (1, 3), (3, 4), (4, 6))
+        w1s = [held([P, S * (e1 - e0), H], U8, f"w1s_{e0}") for e0, e1 in runs]
+        w1_plane = {(e, s): w1s[i][:, S * (e - e0) + s, :] for i, (e0, e1) in enumerate(runs) for e in range(e0, e1) for s in range(S)}
         w2s = held([P, E, N], U8, "w2s")
         y = [held([P, R, E, C // R], F32, f"y{n}") for n in range(N // P)]
         ident = held([P, P], F32, "ident")
@@ -61,22 +57,24 @@ def tile_moe_eps_mlp_relu2_kernel(
         for s in range(1, S):
             nc.sync.dma_start(out=x[s][:], in_=rows(s))
 
-        nc.vector.memset(w1s_a[:].rearrange("p a i -> p (a i)").bitcast(I32), 0)
-        for plane in (scales01, scales23, gb1):
+        for i in (0, 1):
+            nc.vector.memset(w1s[i][:].rearrange("p a i -> p (a i)").bitcast(I32), 0)
+        for plane in (packed, scales23, planes[1]):
             nc.vector.memset(plane[:].bitcast(I32), 0)
-        nc.gpsimd.memset(w1s_b[:].rearrange("p a i -> p (a i)").bitcast(I32), 0)
+        for i in (2, 3):
+            nc.gpsimd.memset(w1s[i][:].rearrange("p a i -> p (a i)").bitcast(I32), 0)
         nc.vector.memset(w2s[:].rearrange("p a i -> p (a i)").bitcast(I32), 0)
         make_identity(nc, ident[:])
 
-        def load_scales(tile, source, parts=1):
-            planes = source.rearrange("e s (b r) i -> r b (e s) i", r=4)
-            width = tile.shape[1] // parts
-            for a in range(0, tile.shape[1], width):
-                for r in range(4):
-                    nc.sync.dma_start(
-                        out=tile[r:P:32, a : a + width, :].bitcast(I32),
-                        in_=planes[r][:, a : a + width, :].bitcast(I32),
-                    )
+        def load_scales(tile, source):
+            for r in range(4):
+                nc.sync.dma_start(
+                    out=tile[r:P:32, :, :].bitcast(I32),
+                    in_=source.rearrange("e s (b r) i -> r b (e s) i", r=4)[r].bitcast(I32),
+                )
+
+        def load_w1_scales(i):
+            load_scales(w1s[i], w1_scales[runs[i][0] : runs[i][1]])
 
         def load_w1(e, tag=None, s0=0, s1=S):
             words = held([P, s1 - s0, 2 * H], U8, f"w1_{e}_{s0}", tag)
@@ -87,21 +85,8 @@ def tile_moe_eps_mlp_relu2_kernel(
             for s in range(s0, s1):
                 w1[e, s] = words[:, s - s0, :]
 
-        def load_first_pair(s):
-            both = held([P, 2, 2 * H], U8, f"w1_pass{s}")
-            nc.sync.dma_start(
-                out=both[:].bitcast(I32),
-                in_=w1_words[0:2, s].rearrange("e p b -> p e b").bitcast(I32),
-            )
-            for e in range(2):
-                w1[e, s] = both[:, e, :]
-
-        load_scales(w1s_a, w1_scales[0:3], 2)
-        for e in range(2):
-            load_w1(e, None, 0, S - 1)
-        load_first_pair(S - 1)
-        load_w1(2)
-        load_scales(w1s_b, w1_scales[3:E], 2)
+        load_w1(0)
+        load_w1_scales(0)
 
         def cast(copy, s, source, c0, c1):
             copy(
@@ -110,7 +95,7 @@ def tile_moe_eps_mlp_relu2_kernel(
             )
 
         def quantize(s):
-            plane = scales01[4 * s : P, :] if s < 2 else scales23[:, T * (s - 2) : T * (s - 1)]
+            plane = packed[4 * s : P, :] if s < 2 else scales23[:, T * (s - 2) : T * (s - 1)]
             nc.vector.quantize_mx(
                 out=codes[:, T * s : T * (s + 1)].bitcast(E4M3),
                 scales=plane,
@@ -120,81 +105,84 @@ def tile_moe_eps_mlp_relu2_kernel(
         def entries(j0, j1):
             return offsets[:, j0 // 16 : j1 // 16]
 
-        def gather_words(g, s, j0, j1, whole):
-            window = codes[:, T * s : (S * T if whole else T * (s + 1))]
-            dst = gw[g][:, PAIR * (s - 1) + j0 : PAIR * (s - 1) + j1]
-            nc.vector.tensor_copy(dst, window.indirect(entries(PAIR * g + j0, PAIR * g + j1)))
+        def gather_words(s, e0, e1, until):
+            dst = held([P, C * (e1 - e0)], U32, f"gw{s}_{e0}")
+            nc.vector.tensor_copy(dst[:], codes[:, T * s : T * (until + 1)].indirect(entries(C * e0, C * e1)))
+            for e in range(e0, e1):
+                gw[e, s] = dst[:, C * (e - e0) : C * (e - e0 + 1)]
 
-        def gather_bytes(g, s, j0, j1, whole):
-            window = scales23[:, T * (s - 2) : (2 * T if whole else T * (s - 1))]
-            dst = gb[g][:, PAIR * (s - 2) + j0 : PAIR * (s - 2) + j1]
-            nc.vector.tensor_copy(dst, window.indirect(entries(PAIR * g + j0, PAIR * g + j1)))
+        def gather_bytes(s, e0, e1, window):
+            dst = held([P, C * (e1 - e0)], U8, f"gb{s}_{e0}")
+            nc.vector.tensor_copy(dst[:], window.indirect(entries(C * e0, C * e1)))
+            for e in range(e0, e1):
+                gb[e, s] = dst[:, C * (e - e0) : C * (e - e0 + 1)]
 
-        for g in range(E // 2):
-            gw[g] = held([P, 3 * PAIR], U32, f"gw_{g}")
-            gb[g] = held([P, 2 * PAIR], U8, f"gb_{g}")
-
-        cast(nc.scalar.copy, 0, x[0], 0, 192)
-        cast(nc.vector.tensor_copy, 0, x[0], 192, T)
-        quantize(0)
-        nc.vector.tensor_copy(gw0[:, 0:384], codes[:, 0:T].indirect(entries(0, 384)))
-        for s in range(1, S):
-            split = (256, 512, 384)[s - 1]
+        def tokens(s, split):
             cast(nc.scalar.copy, s, x[s], 0, split)
             if split < T:
                 cast(nc.vector.tensor_copy, s, x[s], split, T)
             quantize(s)
-            if s == 1:
-                for j in (0, 384):
-                    nc.vector.tensor_copy(gb0[:, j : j + 384], scales01[:].indirect(entries(j, j + 384)))
-        nc.scalar.dma_start(out=gb1[0:112, :].bitcast(I32), in_=gb0[4 : 4 + 112, :].bitcast(I32))
-        gather_words(0, 1, 0, PAIR, False)
-        gather_words(0, 2, 0, PAIR, False)
-        gather_bytes(0, 2, 0, PAIR, False)
-        for j in (0, C):
-            gather_words(0, 3, j, j + C, False)
-            gather_bytes(0, 3, j, j + C, False)
 
-        load_w1(3, "x0")
-        load_w1(4, "xg0")
-        load_w1(5, "x1", 0, S - 1)
-        load_w1(5, "xg1", S - 1, S)
-        w2 = held([P, E, 2 * N], U8, "w2", "x3")
+        tokens(0, 192)
+        gather_words(0, 0, 3, 0)
+        tokens(1, 256)
+        for j in (0, 384):
+            nc.vector.tensor_copy(planes[0][:, j : j + 384], packed[:].indirect(entries(j, j + 384)))
+        nc.sync.dma_start(out=planes[1][0:112, :].bitcast(I32), in_=planes[0][4 : 4 + 112, :].bitcast(I32))
+        load_w1_scales(1)
+        gather_words(1, 0, 2, 1)
+        tokens(2, T)
+        gather_words(2, 0, 2, 2)
+        gather_bytes(2, 0, 2, scales23[:, 0:T])
+        tokens(3, T)
+        for e in range(2):
+            gather_words(3, e, e + 1, 3)
+            gather_bytes(3, e, e + 1, scales23[:, T : 2 * T])
+        gather_bytes(2, 2, 4, scales23[:])
+        for e in (2, 3):
+            gather_words(2, e, e + 1, 3)
+            if e == 2:
+                gather_words(1, 2, 4, 3)
+            else:
+                gather_words(0, 3, E, 3)
+            gather_words(3, e, e + 1, 3)
+            gather_bytes(3, e, e + 1, scales23[:, T : 2 * T])
+        gather_words(1, 4, E, 3)
+        gather_words(2, 4, E, 3)
+        gather_bytes(2, 4, E, scales23[:])
+        for e in (4, 5):
+            gather_words(3, e, e + 1, 3)
+            gather_bytes(3, e, e + 1, scales23[:, T : 2 * T])
+
+        load_w1(1, "x0")
+        load_w1(2, "xg0")
+        load_w1(3, "x1")
+        load_w1_scales(2)
+        load_w1_scales(3)
+        load_w1(4, "xg1", 0, 2)
+        load_w1(4, "packed", 2, S)
+        load_w1(5, "x2", 0, 2)
+        load_w1(5, "xg2", 2, 3)
+        load_w1(5, "x3", 3, S)
+        w2 = held([P, E, 2 * N], U8, "w2", "xg3")
+        nc.sync.dma_start(out=w2[:].bitcast(I32), in_=w2_words.rearrange("e s p b -> p (e s) b").bitcast(I32))
         load_scales(w2s, w2_scales)
-        for e0 in (0, 3):
-            nc.sync.dma_start(
-                out=w2[:, e0 : e0 + 3, :].bitcast(I32),
-                in_=w2_words[e0 : e0 + 3].rearrange("e s p b -> p (e s) b").bitcast(I32),
-            )
-
-        def gather_late(g, j0, j1):
-            for s in range(2, S):
-                gather_words(g, s, j0, j1, True)
-                gather_bytes(g, s, j0, j1, True)
 
         def first(e, a, passes):
-            g, j = divmod(C * e, PAIR)
             for s in passes:
-                if s == 0:
-                    words = gw0[:, C * e : C * (e + 1)]
-                else:
-                    words = gw[g][:, PAIR * (s - 1) + j : PAIR * (s - 1) + j + C]
-                if s < 2:
-                    plane = (gb0, gb1)[s][:, C * e : C * (e + 1)]
-                else:
-                    plane = gb[g][:, PAIR * (s - 2) + j : PAIR * (s - 2) + j + C]
+                plane = planes[s][:, C * e : C * (e + 1)] if s < 2 else gb[e, s]
                 nc.tensor.matmul_mx(
                     out=a[:],
-                    lhsT=words.bitcast(E4M3),
+                    lhsT=gw[e, s].bitcast(E4M3),
                     lhsT_scale=plane,
                     rhs=w1[e, s].bitcast(E2M1),
-                    rhs_scale=w1s_a[:, S * e + s, :] if e < 3 else w1s_b[:, S * (e - 3) + s, :],
-                    start=(s == 0),
-                    stop=(s == (ORDER[-1] if e < 2 else S - 1)),
+                    rhs_scale=w1_plane[e, s],
+                    start=(s == passes[0]),
+                    stop=(s == passes[-1]),
                 )
 
         def relu(e, a):
-            r = work.tile([P, 4, P], F32, name="r", align_bytes=64)
+            r = held([P, 4, P], F32, f"r{e}", {0: "gw1_0", 1: "gw2_2", 2: "gw2_3", 4: "x2"}.get(e))
             step = 2 if e == E - 1 else 4
             for d in range(0, 4, step):
                 nc.scalar.activation(r[:, d : d + step, :], a[:].rearrange("c (p t) -> c t p", t=4)[:, d : d + step, :], RELU)
@@ -229,34 +217,27 @@ def tile_moe_eps_mlp_relu2_kernel(
                 stop=True,
             )
 
-        def results(e0):
-            banks = [psum_y.tile([P, 3, C], F32, name="b") for n in range(N // P)]
-            for e in range(e0, e0 + 3):
+        def results(e0, e1, banks):
+            for e in range(e0, e1):
                 for n in range(N // P):
-                    second(e, n, banks[n][:, e - e0, :])
+                    second(e, n, banks[n][:, e % 3, :])
             for n in range(N // P):
                 copy = nc.scalar.copy if n == 1 else nc.vector.tensor_copy
-                copy(y[n][:, :, e0 : e0 + 3, :], banks[n][:].rearrange("p e (m u) -> p m e u", m=R))
+                copy(y[n][:, :, e0:e1, :], banks[n][:, e0 % 3 : (e1 - 1) % 3 + 1, :].rearrange("p e (m u) -> p m e u", m=R))
 
-        gather_words(1, 1, 0, PAIR, True)
-        gather_late(1, 0, C)
-        nc.vector.tensor_copy(gw0[:, 384:SLOTS], codes[:].indirect(entries(384, SLOTS)))
-        gather_late(1, C, PAIR)
-        gather_words(2, 1, 0, PAIR, True)
-        gather_late(2, 0, C)
-        gather_late(2, C, PAIR)
         a, q = {}, {}
         for e in range(2):
             a[e] = psum_a.tile([P, H], F32, name="a")
-        for passes in (ORDER[:2], ORDER[2:3], ORDER[3:]):
-            first(0, a[0], passes)
-            first(1, a[1], passes)
+            first(e, a[e], range(S))
+        warm = psum_y.tile([P, H], F32, name="b")
+        for i in range(4):
+            first(0, warm, (0,))
         for e in range(E):
             q[e] = quantize_h(e, square(e, turn(relu(e, a[e]))))
             if e + 2 < E:
                 a[e + 2] = psum_a.tile([P, H], F32, name="a")
-                first(e + 2, a[e + 2], range(S))
-        results(0)
-        results(3)
+                first(e + 2, a[e + 2], (2, 0, 1, 3) if e < 2 else range(S))
+        results(0, 3, [psum_y.tile([P, 3, C], F32, name="b") for n in range(N // P)])
+        results(3, 6, [psum_a.tile([P, 3, C], F32, name="a") for n in range(N // P)])
         for n in range(N // P):
             nc.sync.dma_start(out=out[P * n : P * (n + 1), :], in_=y[n][:].rearrange("p m e u -> p (m e u)"))

@@ -27,9 +27,10 @@ def tile_moe_eps_mlp_relu2_kernel(
     nc = tc.nc
     with ExitStack() as ctx:
         keep = ctx.enter_context(tc.tile_pool(name="keep", bufs=1))
-        psum_a = ctx.enter_context(tc.psum_pool(name="psum_a", bufs=3))
-        psum_t = ctx.enter_context(tc.psum_pool(name="psum_t", bufs=2))
-        psum_y = ctx.enter_context(tc.psum_pool(name="psum_y", bufs=3))
+        psum = ctx.enter_context(tc.psum_pool(name="psum", bufs=1))
+
+        def bank(b, name):
+            return psum.tile([P, 4, C], F32, name=name, tag=f"bank{b}")
 
         def held(shape, dtype, name, tag=None):
             return keep.tile(shape, dtype, name=name, tag=tag or name, align_bytes=64)
@@ -40,7 +41,7 @@ def tile_moe_eps_mlp_relu2_kernel(
         codes = held([P, S * T], U32, "codes")
         packed = held([P, T], U8, "packed")
         scales23 = held([P, 2 * T], U8, "scales23")
-        planes = [held([P, SLOTS], U8, f"plane{s}") for s in range(2)]
+        planes = {(s, e0): held([P, 3 * C], U8, f"plane{s}_{e0}") for s in range(2) for e0 in (0, 3)}
         runs = ((0, 1), (1, 3), (3, 4), (4, 6))
         w1s = [held([P, S * (e1 - e0), H], U8, f"w1s_{e0}") for e0, e1 in runs]
         w1_plane = {(e, s): w1s[i][:, S * (e - e0) + s, :] for i, (e0, e1) in enumerate(runs) for e in range(e0, e1) for s in range(S)}
@@ -59,7 +60,7 @@ def tile_moe_eps_mlp_relu2_kernel(
 
         for i in (0, 1):
             nc.vector.memset(w1s[i][:].rearrange("p a i -> p (a i)").bitcast(I32), 0)
-        for plane in (packed, scales23, planes[1]):
+        for plane in (packed, scales23, planes[1, 0], planes[1, 3]):
             nc.vector.memset(plane[:].bitcast(I32), 0)
         for i in (2, 3):
             nc.gpsimd.memset(w1s[i][:].rearrange("p a i -> p (a i)").bitcast(I32), 0)
@@ -123,12 +124,16 @@ def tile_moe_eps_mlp_relu2_kernel(
                 cast(nc.vector.tensor_copy, s, x[s], split, T)
             quantize(s)
 
+        def move_plane(e0):
+            nc.sync.dma_start(out=planes[1, e0][0:112, :].bitcast(I32), in_=planes[0, e0][4 : 4 + 112, :].bitcast(I32))
+
         tokens(0, 192)
-        gather_words(0, 0, 3, 0)
-        tokens(1, 256)
-        for j in (0, 384):
-            nc.vector.tensor_copy(planes[0][:, j : j + 384], packed[:].indirect(entries(j, j + 384)))
-        nc.sync.dma_start(out=planes[1][0:112, :].bitcast(I32), in_=planes[0][4 : 4 + 112, :].bitcast(I32))
+        for e0 in (0, 3):
+            gather_words(0, e0, e0 + 3, 0)
+        tokens(1, 320)
+        for e0 in (0, 3):
+            nc.vector.tensor_copy(planes[0, e0][:], packed[:].indirect(entries(C * e0, C * (e0 + 3))))
+        move_plane(0)
         load_w1_scales(1)
         gather_words(1, 0, 2, 1)
         tokens(2, T)
@@ -138,31 +143,25 @@ def tile_moe_eps_mlp_relu2_kernel(
         for e in range(2):
             gather_words(3, e, e + 1, 3)
             gather_bytes(3, e, e + 1, scales23[:, T : 2 * T])
-        gather_bytes(2, 2, 4, scales23[:])
-        for e in (2, 3):
-            gather_words(2, e, e + 1, 3)
-            if e == 2:
-                gather_words(1, 2, 4, 3)
-            else:
-                gather_words(0, 3, E, 3)
-            gather_words(3, e, e + 1, 3)
-            gather_bytes(3, e, e + 1, scales23[:, T : 2 * T])
-        gather_words(1, 4, E, 3)
-        gather_words(2, 4, E, 3)
-        gather_bytes(2, 4, E, scales23[:])
-        for e in (4, 5):
-            gather_words(3, e, e + 1, 3)
-            gather_bytes(3, e, e + 1, scales23[:, T : 2 * T])
+        for e0 in (2, 4):
+            gather_bytes(2, e0, e0 + 2, scales23[:])
+            for e in (e0, e0 + 1):
+                gather_words(2, e, e + 1, 3)
+                if e == e0:
+                    gather_words(1, e0, e0 + 2, 3)
+                gather_words(3, e, e + 1, 3)
+                gather_bytes(3, e, e + 1, scales23[:, T : 2 * T])
 
         load_w1(1, "x0")
+        move_plane(3)
         load_w1(2, "xg0")
         load_w1(3, "x1")
         load_w1_scales(2)
         load_w1_scales(3)
-        load_w1(4, "xg1", 0, 2)
-        load_w1(4, "packed", 2, S)
-        load_w1(5, "x2", 0, 2)
-        load_w1(5, "xg2", 2, 3)
+        load_w1(4, "xg1", 0, 1)
+        load_w1(4, "packed", 1, S)
+        load_w1(5, "x2", 0, 1)
+        load_w1(5, "xg2", 1, 3)
         load_w1(5, "x3", 3, S)
         w2 = held([P, E, 2 * N], U8, "w2", "xg3")
         nc.sync.dma_start(out=w2[:].bitcast(I32), in_=w2_words.rearrange("e s p b -> p (e s) b").bitcast(I32))
@@ -170,9 +169,9 @@ def tile_moe_eps_mlp_relu2_kernel(
 
         def first(e, a, passes):
             for s in passes:
-                plane = planes[s][:, C * e : C * (e + 1)] if s < 2 else gb[e, s]
+                plane = planes[s, e // 3 * 3][:, C * (e % 3) : C * (e % 3 + 1)] if s < 2 else gb[e, s]
                 nc.tensor.matmul_mx(
-                    out=a[:],
+                    out=a[:].rearrange("p d c -> p (d c)"),
                     lhsT=gw[e, s].bitcast(E4M3),
                     lhsT_scale=plane,
                     rhs=w1[e, s].bitcast(E2M1),
@@ -182,14 +181,13 @@ def tile_moe_eps_mlp_relu2_kernel(
                 )
 
         def relu(e, a):
-            r = held([P, 4, P], F32, f"r{e}", {0: "gw1_0", 1: "gw2_2", 2: "gw2_3", 4: "x2"}.get(e))
+            r = held([P, 4, P], F32, f"r{e}", {0: "gw1_0", 2: "gw2_3", 4: "x2"}.get(e))
             step = 2 if e == E - 1 else 4
             for d in range(0, 4, step):
-                nc.scalar.activation(r[:, d : d + step, :], a[:].rearrange("c (p t) -> c t p", t=4)[:, d : d + step, :], RELU)
+                nc.scalar.activation(r[:, d : d + step, :], a[:].rearrange("c u (v t) -> c t (u v)", t=4)[:, d : d + step, :], RELU)
             return r
 
-        def turn(r):
-            t = psum_t.tile([P, 4, C], F32, name="t")
+        def turn(r, t):
             for d in range(4):
                 nc.tensor.transpose(t[:, d, :], r[:, d, :], ident[:])
             return t
@@ -225,19 +223,36 @@ def tile_moe_eps_mlp_relu2_kernel(
                 copy = nc.scalar.copy if n == 1 else nc.vector.tensor_copy
                 copy(y[n][:, :, e0:e1, :], banks[n][:, e0 % 3 : (e1 - 1) % 3 + 1, :].rearrange("p e (m u) -> p m e u", m=R))
 
-        a, q = {}, {}
-        for e in range(2):
-            a[e] = psum_a.tile([P, H], F32, name="a")
-            first(e, a[e], range(S))
-        warm = psum_y.tile([P, H], F32, name="b")
+        a, r, q = {}, {}, {}
+
+        def product(e, b, passes):
+            a[e] = bank(b, f"a{e}")
+            first(e, a[e], passes)
+
+        def finish(e, b):
+            q[e] = quantize_h(e, square(e, turn(r[e], bank(b, f"t{e}"))))
+
+        product(0, 0, range(S))
+        product(1, 1, range(S))
+        warm = bank(4, "warm")
         for i in range(4):
             first(0, warm, (0,))
-        for e in range(E):
-            q[e] = quantize_h(e, square(e, turn(relu(e, a[e]))))
-            if e + 2 < E:
-                a[e + 2] = psum_a.tile([P, H], F32, name="a")
-                first(e + 2, a[e + 2], (2, 0, 1, 3) if e < 2 else range(S))
-        results(0, 3, [psum_y.tile([P, 3, C], F32, name="b") for n in range(N // P)])
-        results(3, 6, [psum_a.tile([P, 3, C], F32, name="a") for n in range(N // P)])
+        r[0] = relu(0, a[0])
+        finish(0, 4)
+        product(2, 2, (2, 0, 1, 3))
+        r[1] = relu(1, a[1])
+        product(3, 3, (2, 0, 1, 3))
+        for e in (2, 3):
+            r[e] = relu(e, a[e])
+        for e, b in ((1, 2), (2, 0), (3, 1)):
+            finish(e, b)
+        product(4, 5, range(S))
+        product(5, 6, range(S))
+        for e in (4, 5):
+            r[e] = relu(e, a[e])
+        for e, b in ((4, 7), (5, 3)):
+            finish(e, b)
+        results(0, 3, [bank(b, f"y{b}") for b in (4, 2, 0)])
+        results(3, 6, [bank(b, f"y{b}") for b in (1, 5, 6)])
         for n in range(N // P):
             nc.sync.dma_start(out=out[P * n : P * (n + 1), :], in_=y[n][:].rearrange("p m e u -> p (m e u)"))

@@ -86,7 +86,7 @@ def tile_moe_eps_mlp_relu2_kernel(
             for s in range(s0, s1):
                 w1[e, s] = words[:, s - s0, :]
 
-        load_w1(0)
+        load_w1(0, None, 0, S - 1)
         load_w1_scales(0)
 
         def cast(copy, s, source, c0, c1):
@@ -152,7 +152,13 @@ def tile_moe_eps_mlp_relu2_kernel(
                 gather_words(3, e, e + 1, 3)
                 gather_bytes(3, e, e + 1, scales23[:, T : 2 * T])
 
-        load_w1(1, "x0")
+        load_w1(1, "x0", 0, S - 1)
+        both = held([P, 2, 2 * H], U8, "w1_last_pass")
+        nc.sync.dma_start(
+            out=both[:].bitcast(I32), in_=w1_words[0:2, S - 1].rearrange("e p b -> p e b").bitcast(I32)
+        )
+        for e in range(2):
+            w1[e, S - 1] = both[:, e, :]
         move_plane(3)
         load_w1(2, "xg0")
         load_w1(3, "x1")
@@ -181,7 +187,7 @@ def tile_moe_eps_mlp_relu2_kernel(
                 )
 
         def relu(e, a):
-            r = held([P, 4, P], F32, f"r{e}", {0: "gw1_0", 2: "gw2_3", 4: "x2"}.get(e))
+            r = held([P, 4, P], F32, f"r{e}", {2: "gw2_3", 4: "x2"}.get(e))
             step = 2 if e == E - 1 else 4
             for d in range(0, 4, step):
                 nc.scalar.activation(r[:, d : d + step, :], a[:].rearrange("c u (v t) -> c t (u v)", t=4)[:, d : d + step, :], RELU)
@@ -215,13 +221,8 @@ def tile_moe_eps_mlp_relu2_kernel(
                 stop=True,
             )
 
-        def results(e0, e1, banks):
-            for e in range(e0, e1):
-                for n in range(N // P):
-                    second(e, n, banks[n][:, e % 3, :])
-            for n in range(N // P):
-                copy = nc.scalar.copy if n == 1 else nc.vector.tensor_copy
-                copy(y[n][:, :, e0:e1, :], banks[n][:, e0 % 3 : (e1 - 1) % 3 + 1, :].rearrange("p e (m u) -> p m e u", m=R))
+        def collect(copy, n, e0, b):
+            copy(y[n][:, :, e0 : e0 + 3, :], b[:, 0:3, :].rearrange("p e (m u) -> p m e u", m=R))
 
         a, r, q = {}, {}, {}
 
@@ -234,9 +235,6 @@ def tile_moe_eps_mlp_relu2_kernel(
 
         product(0, 0, range(S))
         product(1, 1, range(S))
-        warm = bank(4, "warm")
-        for i in range(4):
-            first(0, warm, (0,))
         r[0] = relu(0, a[0])
         finish(0, 4)
         product(2, 2, (2, 0, 1, 3))
@@ -252,7 +250,16 @@ def tile_moe_eps_mlp_relu2_kernel(
             r[e] = relu(e, a[e])
         for e, b in ((4, 7), (5, 3)):
             finish(e, b)
-        results(0, 3, [bank(b, f"y{b}") for b in (4, 2, 0)])
-        results(3, 6, [bank(b, f"y{b}") for b in (1, 5, 6)])
+        for n, b in enumerate((4, 2, 0)):
+            early = bank(b, f"early{n}")
+            for e in range(3):
+                second(e, n, early[:, e, :])
+            collect(nc.vector.tensor_copy if n == 0 else nc.scalar.copy, n, 0, early)
+        late = [bank(b, f"late{b}") for b in (1, 5, 6)]
+        for e in range(3, E):
+            for n in range(N // P):
+                second(e, n, late[n][:, e - 3, :])
+        for n in range(N // P):
+            collect(nc.scalar.copy if n == 1 else nc.vector.tensor_copy, n, 3, late[n])
         for n in range(N // P):
             nc.sync.dma_start(out=out[P * n : P * (n + 1), :], in_=y[n][:].rearrange("p m e u -> p (m e u)"))

@@ -20,6 +20,9 @@ E2M1 = mybir.dt.float4_e2m1fn_x4
 RELU = mybir.ActivationFunctionType.Relu
 SQUARE = mybir.ActivationFunctionType.Square
 
+SCALAR_TOKENS = (192, 320, 512, 416)
+WORD_LOADS = (((0, 1), (1, 4)),) + (((0, 1), (1, 3), (3, 4)),) * 4 + (((0, 2), (2, 4)),)
+
 
 def tile_moe_eps_mlp_relu2_kernel(
     tc, xT, w1_words, w1_scales, w2_words, w2_scales, offs, out
@@ -27,28 +30,34 @@ def tile_moe_eps_mlp_relu2_kernel(
     nc = tc.nc
     with ExitStack() as ctx:
         keep = ctx.enter_context(tc.tile_pool(name="keep", bufs=1))
+        slab = ctx.enter_context(tc.tile_pool(name="slab", bufs=1))
         psum = ctx.enter_context(tc.psum_pool(name="psum", bufs=1))
 
         def bank(b, name):
             return psum.tile([P, 4, C], F32, name=name, tag=f"bank{b}")
 
-        def held(shape, dtype, name, tag=None):
-            return keep.tile(shape, dtype, name=name, tag=tag or name, align_bytes=64)
+        def held(shape, dtype, name):
+            return keep.tile(shape, dtype, name=name, align_bytes=64)
+
+        def placed(shape, dtype, name, offset):
+            return slab.tile(shape, dtype, name=name, align_bytes=64, offset=offset)
+
+        used = [0]
+
+        def over_tokens(shape, name, size):
+            tile = placed(shape, U8, name, used[0])
+            used.append(used.pop() + size)
+            return tile
 
         offsets = keep.tile([P, SLOTS // 16], U16, name="offsets")
-        x = [held([P, 4, T], F32, f"x{s}") for s in range(S)]
-        xg = [held([P, T, 4], BF16, f"xg{s}") for s in range(S)]
+        x = [placed([P, 4, T], F32, f"x{s}", 24 * T * s) for s in range(S)]
+        xg = [placed([P, T, 4], BF16, f"xg{s}", 24 * T * s + 16 * T) for s in range(S)]
         codes = held([P, S * T], U32, "codes")
-        packed = held([P, T], U8, "packed")
-        scales23 = held([P, 2 * T], U8, "scales23")
-        planes = {(s, e0): held([P, 3 * C], U8, f"plane{s}_{e0}") for s in range(2) for e0 in (0, 3)}
-        runs = ((0, 1), (1, 3), (3, 4), (4, 6))
-        w1s = [held([P, S * (e1 - e0), H], U8, f"w1s_{e0}") for e0, e1 in runs]
-        w1_plane = {(e, s): w1s[i][:, S * (e - e0) + s, :] for i, (e0, e1) in enumerate(runs) for e in range(e0, e1) for s in range(S)}
-        w2s = held([P, E, N], U8, "w2s")
+        token_scales = held([P, 3 * T], U8, "token_scales")
+        planes = [held([P, SLOTS], U8, f"plane{s}") for s in range(2)]
         y = [held([P, R, E, C // R], F32, f"y{n}") for n in range(N // P)]
         ident = held([P, P], F32, "ident")
-        w1, gw, gb = {}, {}, {}
+        w1, w1s, w2, gw, gb, first_place = {}, {}, {}, {}, {}, {}
 
         def rows(s):
             return xT[512 * s : 512 * (s + 1), :].rearrange("(p j) w -> p j w", j=4)
@@ -58,13 +67,8 @@ def tile_moe_eps_mlp_relu2_kernel(
         for s in range(1, S):
             nc.sync.dma_start(out=x[s][:], in_=rows(s))
 
-        for i in (0, 1):
-            nc.vector.memset(w1s[i][:].rearrange("p a i -> p (a i)").bitcast(I32), 0)
-        for plane in (packed, scales23, planes[1, 0], planes[1, 3]):
+        for plane in (token_scales, planes[1]):
             nc.vector.memset(plane[:].bitcast(I32), 0)
-        for i in (2, 3):
-            nc.gpsimd.memset(w1s[i][:].rearrange("p a i -> p (a i)").bitcast(I32), 0)
-        nc.vector.memset(w2s[:].rearrange("p a i -> p (a i)").bitcast(I32), 0)
         make_identity(nc, ident[:])
 
         def load_scales(tile, source):
@@ -74,11 +78,16 @@ def tile_moe_eps_mlp_relu2_kernel(
                     in_=source.rearrange("e s (b r) i -> r b (e s) i", r=4)[r].bitcast(I32),
                 )
 
-        def load_w1_scales(i):
-            load_scales(w1s[i], w1_scales[runs[i][0] : runs[i][1]])
+        def load_w1_scales(e):
+            w1s[e] = over_tokens([P, S, H], f"w1s_{e}", S * H)
+            load_scales(w1s[e], w1_scales[e : e + 1])
 
-        def load_w1(e, tag=None, s0=0, s1=S):
-            words = held([P, s1 - s0, 2 * H], U8, f"w1_{e}_{s0}", tag)
+        def load_w1(e, piece):
+            s0, s1 = WORD_LOADS[e][piece]
+            if piece == 0:
+                first_place[e] = used[0]
+            size = 4 * H if piece == 0 and e > 0 else 2 * H * (s1 - s0)
+            words = over_tokens([P, s1 - s0, 2 * H], f"w1_{e}_{s0}", size)
             nc.sync.dma_start(
                 out=words[:].bitcast(I32),
                 in_=w1_words[e, s0:s1].rearrange("s p b -> p s b").bitcast(I32),
@@ -86,134 +95,121 @@ def tile_moe_eps_mlp_relu2_kernel(
             for s in range(s0, s1):
                 w1[e, s] = words[:, s - s0, :]
 
-        load_w1(0, None, 0, S - 1)
-        load_w1_scales(0)
+        def load_w2(e0):
+            words = over_tokens([P, 3, 2 * N], f"w2_{e0}", 6 * N)
+            nc.sync.dma_start(
+                out=words[:].bitcast(I32),
+                in_=w2_words[e0 : e0 + 3].rearrange("e s p b -> p (e s) b").bitcast(I32),
+            )
+            for e in range(e0, e0 + 3):
+                w2[e] = words[:, e - e0, :]
 
-        def cast(copy, s, source, c0, c1):
+        def cast(copy, s, c0, c1):
             copy(
                 out=xg[s][:, c0:c1, :].rearrange("p (c i) j -> p c j i", i=4),
-                in_=source[:, :, c0:c1].rearrange("p j (c i) -> p c j i", i=4),
+                in_=x[s][:, :, c0:c1].rearrange("p j (c i) -> p c j i", i=4),
             )
 
-        def quantize(s):
-            plane = packed[4 * s : P, :] if s < 2 else scales23[:, T * (s - 2) : T * (s - 1)]
+        def tokens(s):
+            cast(nc.scalar.copy, s, 0, SCALAR_TOKENS[s])
+            if SCALAR_TOKENS[s] < T:
+                cast(nc.vector.tensor_copy, s, SCALAR_TOKENS[s], T)
+            plane = token_scales[4 * s : P, 0:T] if s < 2 else token_scales[:, T * (s - 1) : T * s]
             nc.vector.quantize_mx(
                 out=codes[:, T * s : T * (s + 1)].bitcast(E4M3),
                 scales=plane,
                 in_=xg[s][:].rearrange("p w j -> p (w j)"),
             )
 
-        def entries(j0, j1):
-            return offsets[:, j0 // 16 : j1 // 16]
+        def entries(e0, e1):
+            return offsets[:, C * e0 // 16 : C * e1 // 16]
 
         def gather_words(s, e0, e1, until):
             dst = held([P, C * (e1 - e0)], U32, f"gw{s}_{e0}")
-            nc.vector.tensor_copy(dst[:], codes[:, T * s : T * (until + 1)].indirect(entries(C * e0, C * e1)))
+            nc.vector.tensor_copy(dst[:], codes[:, T * s : T * (until + 1)].indirect(entries(e0, e1)))
             for e in range(e0, e1):
                 gw[e, s] = dst[:, C * (e - e0) : C * (e - e0 + 1)]
 
-        def gather_bytes(s, e0, e1, window):
+        def gather_bytes(s, e0, e1, until):
             dst = held([P, C * (e1 - e0)], U8, f"gb{s}_{e0}")
-            nc.vector.tensor_copy(dst[:], window.indirect(entries(C * e0, C * e1)))
+            nc.vector.tensor_copy(dst[:], token_scales[:, T * (s - 1) : T * until].indirect(entries(e0, e1)))
             for e in range(e0, e1):
                 gb[e, s] = dst[:, C * (e - e0) : C * (e - e0 + 1)]
 
-        def tokens(s, split):
-            cast(nc.scalar.copy, s, x[s], 0, split)
-            if split < T:
-                cast(nc.vector.tensor_copy, s, x[s], split, T)
-            quantize(s)
-
-        def move_plane(e0):
-            nc.sync.dma_start(out=planes[1, e0][0:112, :].bitcast(I32), in_=planes[0, e0][4 : 4 + 112, :].bitcast(I32))
-
-        tokens(0, 192)
+        tokens(0)
         for e0 in (0, 3):
             gather_words(0, e0, e0 + 3, 0)
-        tokens(1, 320)
+        tokens(1)
         for e0 in (0, 3):
-            nc.vector.tensor_copy(planes[0, e0][:], packed[:].indirect(entries(C * e0, C * (e0 + 3))))
-        move_plane(0)
-        load_w1_scales(1)
+            nc.vector.tensor_copy(planes[0][:, C * e0 : C * (e0 + 3)], token_scales[:, 0:T].indirect(entries(e0, e0 + 3)))
         gather_words(1, 0, 2, 1)
-        tokens(2, T)
+        tokens(2)
         gather_words(2, 0, 2, 2)
-        gather_bytes(2, 0, 2, scales23[:, 0:T])
-        tokens(3, T)
+        gather_bytes(2, 0, 2, 2)
+        tokens(3)
         for e in range(2):
             gather_words(3, e, e + 1, 3)
-            gather_bytes(3, e, e + 1, scales23[:, T : 2 * T])
+            gather_bytes(3, e, e + 1, 3)
         for e0 in (2, 4):
-            gather_bytes(2, e0, e0 + 2, scales23[:])
+            gather_words(1, e0, e0 + 2, 3)
+            gather_bytes(2, e0, e0 + 2, 3)
             for e in (e0, e0 + 1):
                 gather_words(2, e, e + 1, 3)
-                if e == e0:
-                    gather_words(1, e0, e0 + 2, 3)
                 gather_words(3, e, e + 1, 3)
-                gather_bytes(3, e, e + 1, scales23[:, T : 2 * T])
+                gather_bytes(3, e, e + 1, 3)
 
-        load_w1(1, "x0", 0, S - 1)
-        both = held([P, 2, 2 * H], U8, "w1_last_pass")
-        nc.sync.dma_start(
-            out=both[:].bitcast(I32), in_=w1_words[0:2, S - 1].rearrange("e p b -> p e b").bitcast(I32)
-        )
-        for e in range(2):
-            w1[e, S - 1] = both[:, e, :]
-        move_plane(3)
-        load_w1(2, "xg0")
-        load_w1(3, "x1")
-        load_w1_scales(2)
-        load_w1_scales(3)
-        load_w1(4, "xg1", 0, 1)
-        load_w1(4, "packed", 1, S)
-        load_w1(5, "x2", 0, 1)
-        load_w1(5, "xg2", 1, 3)
-        load_w1(5, "x3", 3, S)
-        w2 = held([P, E, 2 * N], U8, "w2", "xg3")
-        nc.sync.dma_start(out=w2[:].bitcast(I32), in_=w2_words.rearrange("e s p b -> p (e s) b").bitcast(I32))
+        for e in range(E):
+            load_w1_scales(e)
+            for piece in range(len(WORD_LOADS[e])):
+                load_w1(e, piece)
+            if e == 0:
+                nc.sync.dma_start(out=planes[1][0:112, :].bitcast(I32), in_=planes[0][4 : 4 + 112, :].bitcast(I32))
+        w2s = over_tokens([P, E, N], "w2s", E * N)
         load_scales(w2s, w2_scales)
+        load_w2(0)
+        load_w2(3)
 
-        def first(e, a, passes):
-            for s in passes:
-                plane = planes[s, e // 3 * 3][:, C * (e % 3) : C * (e % 3 + 1)] if s < 2 else gb[e, s]
+        a, q = {}, {}
+
+        def product(e):
+            a[e] = bank(e % 3, f"a{e}")
+            for s in range(S):
+                plane = planes[s][:, C * e : C * (e + 1)] if s < 2 else gb[e, s]
                 nc.tensor.matmul_mx(
-                    out=a[:].rearrange("p d c -> p (d c)"),
+                    out=a[e][:].rearrange("p d c -> p (d c)"),
                     lhsT=gw[e, s].bitcast(E4M3),
                     lhsT_scale=plane,
                     rhs=w1[e, s].bitcast(E2M1),
-                    rhs_scale=w1_plane[e, s],
-                    start=(s == passes[0]),
-                    stop=(s == passes[-1]),
+                    rhs_scale=w1s[e][:, s, :],
+                    start=(s == 0),
+                    stop=(s == S - 1),
                 )
 
-        def relu(e, a):
-            r = held([P, 4, P], F32, f"r{e}", {2: "gw2_3", 4: "x2"}.get(e))
-            step = 2 if e == E - 1 else 4
-            for d in range(0, 4, step):
-                nc.scalar.activation(r[:, d : d + step, :], a[:].rearrange("c u (v t) -> c t (u v)", t=4)[:, d : d + step, :], RELU)
-            return r
-
-        def turn(r, t):
+        def hidden(e):
+            if e + 1 < E:
+                r = placed([P, 4, P], F32, f"r{e}", first_place[e + 1])
+            else:
+                r = held([P, 4, P], F32, f"r{e}")
+            sums = a[e][:].rearrange("c u (v t) -> c t (u v)", t=4)
+            if e + 1 < E:
+                nc.scalar.activation(r[:], sums, RELU)
+            else:
+                nc.vector.tensor_scalar_max(r[:], sums, 0.0)
+            t = bank(3 + e % 2, f"t{e}")
             for d in range(4):
                 nc.tensor.transpose(t[:, d, :], r[:, d, :], ident[:])
-            return t
-
-        def square(e, t):
             h = held([P, C, 4], BF16, f"h{e}")
             nc.scalar.activation(h[:], t[:].rearrange("p t c -> p c t"), SQUARE)
-            return h
-
-        def quantize_h(e, h):
             hc = held([P, C], U32, f"hc{e}")
             hs = held([P, C], U8, f"hs{e}")
             nc.vector.quantize_mx(out=hc[:].bitcast(E4M3), scales=hs[:], in_=h[:].rearrange("p c t -> p (c t)"))
-            return hc, hs
+            q[e] = hc, hs
 
         def second(e, n, b):
             hc, hs = q[e]
             nc.tensor.matmul_mx(
                 out=b,
-                lhsT=w2[:, e, 2 * P * n : 2 * P * (n + 1)].bitcast(E2M1),
+                lhsT=w2[e][:, 2 * P * n : 2 * P * (n + 1)].bitcast(E2M1),
                 lhsT_scale=w2s[:, e, P * n : P * (n + 1)],
                 rhs=hc[:].bitcast(E4M3),
                 rhs_scale=hs[:],
@@ -221,45 +217,19 @@ def tile_moe_eps_mlp_relu2_kernel(
                 stop=True,
             )
 
-        def collect(copy, n, e0, b):
-            copy(y[n][:, :, e0 : e0 + 3, :], b[:, 0:3, :].rearrange("p e (m u) -> p m e u", m=R))
-
-        a, r, q = {}, {}, {}
-
-        def product(e, b, passes):
-            a[e] = bank(b, f"a{e}")
-            first(e, a[e], passes)
-
-        def finish(e, b):
-            q[e] = quantize_h(e, square(e, turn(r[e], bank(b, f"t{e}"))))
-
-        product(0, 0, range(S))
-        product(1, 1, range(S))
-        r[0] = relu(0, a[0])
-        finish(0, 4)
-        product(2, 2, (2, 0, 1, 3))
-        r[1] = relu(1, a[1])
-        product(3, 3, (2, 0, 1, 3))
-        for e in (2, 3):
-            r[e] = relu(e, a[e])
-        for e, b in ((1, 2), (2, 0), (3, 1)):
-            finish(e, b)
-        product(4, 5, range(S))
-        product(5, 6, range(S))
-        for e in (4, 5):
-            r[e] = relu(e, a[e])
-        for e, b in ((4, 7), (5, 3)):
-            finish(e, b)
-        for n, b in enumerate((4, 2, 0)):
-            early = bank(b, f"early{n}")
-            for e in range(3):
-                second(e, n, early[:, e, :])
-            collect(nc.vector.tensor_copy if n == 0 else nc.scalar.copy, n, 0, early)
-        late = [bank(b, f"late{b}") for b in (1, 5, 6)]
-        for e in range(3, E):
+        def results(copy, e0, b0):
             for n in range(N // P):
-                second(e, n, late[n][:, e - 3, :])
-        for n in range(N // P):
-            collect(nc.scalar.copy if n == 1 else nc.vector.tensor_copy, n, 3, late[n])
+                b = bank(b0 + n, f"y{e0}_{n}")
+                for e in range(e0, e0 + 3):
+                    second(e, n, b[:, e - e0, :])
+                copy(y[n][:, :, e0 : e0 + 3, :], b[:, 0:3, :].rearrange("p e (m u) -> p m e u", m=R))
+
+        product(0)
+        for e in range(1, E):
+            product(e)
+            hidden(e - 1)
+        hidden(E - 1)
+        results(nc.vector.tensor_copy, 0, 2)
+        results(nc.scalar.copy, 3, 5)
         for n in range(N // P):
             nc.sync.dma_start(out=out[P * n : P * (n + 1), :], in_=y[n][:].rearrange("p m e u -> p (m e u)"))

@@ -22,6 +22,8 @@ SQUARE = mybir.ActivationFunctionType.Square
 
 SCALAR_TOKENS = (192, 320, 512, 416)
 WORD_LOADS = (((0, 1), (1, 4)),) + (((0, 1), (1, 3), (3, 4)),) * 4 + (((0, 2), (2, 4)),)
+SUM_BANKS = (0, 1, 2, 3, 5, 6)
+TURN_BANKS = (4, 2, 0, 1, 7, 3)
 
 
 def tile_moe_eps_mlp_relu2_kernel(
@@ -86,7 +88,7 @@ def tile_moe_eps_mlp_relu2_kernel(
             s0, s1 = WORD_LOADS[e][piece]
             if piece == 0:
                 first_place[e] = used[0]
-            size = 4 * H if piece == 0 and e > 0 else 2 * H * (s1 - s0)
+            size = 4 * H if piece == 0 and e % 2 else 2 * H * (s1 - s0)
             words = over_tokens([P, s1 - s0, 2 * H], f"w1_{e}_{s0}", size)
             nc.sync.dma_start(
                 out=words[:].bitcast(I32),
@@ -172,7 +174,7 @@ def tile_moe_eps_mlp_relu2_kernel(
         a, q = {}, {}
 
         def product(e):
-            a[e] = bank(e % 3, f"a{e}")
+            a[e] = bank(SUM_BANKS[e], f"a{e}")
             for s in range(S):
                 plane = planes[s][:, C * e : C * (e + 1)] if s < 2 else gb[e, s]
                 nc.tensor.matmul_mx(
@@ -185,8 +187,8 @@ def tile_moe_eps_mlp_relu2_kernel(
                     stop=(s == S - 1),
                 )
 
-        def hidden(e):
-            if e + 1 < E:
+        def relu(e):
+            if e % 2 == 0:
                 r = placed([P, 4, P], F32, f"r{e}", first_place[e + 1])
             else:
                 r = held([P, 4, P], F32, f"r{e}")
@@ -195,7 +197,10 @@ def tile_moe_eps_mlp_relu2_kernel(
                 nc.scalar.activation(r[:], sums, RELU)
             else:
                 nc.vector.tensor_scalar_max(r[:], sums, 0.0)
-            t = bank(3 + e % 2, f"t{e}")
+            return r
+
+        def turn(e, r):
+            t = bank(TURN_BANKS[e], f"t{e}")
             for d in range(4):
                 nc.tensor.transpose(t[:, d, :], r[:, d, :], ident[:])
             h = held([P, C, 4], BF16, f"h{e}")
@@ -217,19 +222,30 @@ def tile_moe_eps_mlp_relu2_kernel(
                 stop=True,
             )
 
-        def results(copy, e0, b0):
+        def results(copy, e0, banks):
             for n in range(N // P):
-                b = bank(b0 + n, f"y{e0}_{n}")
+                b = bank(banks[n], f"y{e0}_{n}")
                 for e in range(e0, e0 + 3):
                     second(e, n, b[:, e - e0, :])
                 copy(y[n][:, :, e0 : e0 + 3, :], b[:, 0:3, :].rearrange("p e (m u) -> p m e u", m=R))
 
         product(0)
-        for e in range(1, E):
-            product(e)
-            hidden(e - 1)
-        hidden(E - 1)
-        results(nc.vector.tensor_copy, 0, 2)
-        results(nc.scalar.copy, 3, 5)
+        product(1)
+        turn(0, relu(0))
+        product(2)
+        r = {1: relu(1)}
+        product(3)
+        for e in (2, 3):
+            r[e] = relu(e)
+        for e in (1, 2, 3):
+            turn(e, r[e])
+        product(4)
+        product(5)
+        for e in (4, 5):
+            r[e] = relu(e)
+        for e in (4, 5):
+            turn(e, r[e])
+        results(nc.vector.tensor_copy, 0, (6, 7, 3))
+        results(nc.scalar.copy, 3, (4, 2, 0))
         for n in range(N // P):
             nc.sync.dma_start(out=out[P * n : P * (n + 1), :], in_=y[n][:].rearrange("p m e u -> p (m e u)"))

@@ -20,10 +20,10 @@ E2M1 = mybir.dt.float4_e2m1fn_x4
 RELU = mybir.ActivationFunctionType.Relu
 SQUARE = mybir.ActivationFunctionType.Square
 
-SCALAR_TOKENS = (192, 320, 512, 416)
-WORD_LOADS = (((0, 1), (1, 4)),) + (((0, 1), (1, 3), (3, 4)),) * 4 + (((0, 2), (2, 4)),)
+SCALAR_TOKENS = (192, 256, 512, 512)
 SUM_BANKS = (0, 1, 2, 3, 5, 6)
 TURN_BANKS = (4, 2, 0, 1, 7, 3)
+PASS_ORDER = (range(S), range(S), range(S), (1, 0, 2, 3), range(S), range(S))
 
 
 def tile_moe_eps_mlp_relu2_kernel(
@@ -38,8 +38,8 @@ def tile_moe_eps_mlp_relu2_kernel(
         def bank(b, name):
             return psum.tile([P, 4, C], F32, name=name, tag=f"bank{b}")
 
-        def held(shape, dtype, name):
-            return keep.tile(shape, dtype, name=name, align_bytes=64)
+        def held(shape, dtype, name, tag=None):
+            return keep.tile(shape, dtype, name=name, tag=tag or name, align_bytes=64)
 
         def placed(shape, dtype, name, offset):
             return slab.tile(shape, dtype, name=name, align_bytes=64, offset=offset)
@@ -56,10 +56,10 @@ def tile_moe_eps_mlp_relu2_kernel(
         xg = [placed([P, T, 4], BF16, f"xg{s}", 24 * T * s + 16 * T) for s in range(S)]
         codes = held([P, S * T], U32, "codes")
         token_scales = held([P, 3 * T], U8, "token_scales")
-        planes = [held([P, SLOTS], U8, f"plane{s}") for s in range(2)]
+        planes = {(s, e0): held([P, 3 * C], U8, f"plane{s}_{e0}") for s in range(2) for e0 in (0, 3)}
         y = [held([P, R, E, C // R], F32, f"y{n}") for n in range(N // P)]
         ident = held([P, P], F32, "ident")
-        w1, w1s, w2, gw, gb, first_place = {}, {}, {}, {}, {}, {}
+        w1, w1s, gw, gb, relu4_place = {}, {}, {}, {}, []
 
         def rows(s):
             return xT[512 * s : 512 * (s + 1), :].rearrange("(p j) w -> p j w", j=4)
@@ -69,7 +69,7 @@ def tile_moe_eps_mlp_relu2_kernel(
         for s in range(1, S):
             nc.sync.dma_start(out=x[s][:], in_=rows(s))
 
-        for plane in (token_scales, planes[1]):
+        for plane in (token_scales, planes[1, 0], planes[1, 3]):
             nc.vector.memset(plane[:].bitcast(I32), 0)
         make_identity(nc, ident[:])
 
@@ -80,16 +80,20 @@ def tile_moe_eps_mlp_relu2_kernel(
                     in_=source.rearrange("e s (b r) i -> r b (e s) i", r=4)[r].bitcast(I32),
                 )
 
-        def load_w1_scales(e):
-            w1s[e] = over_tokens([P, S, H], f"w1s_{e}", S * H)
-            load_scales(w1s[e], w1_scales[e : e + 1])
+        def load_w1_scales(e0, e1):
+            tile = over_tokens([P, S * (e1 - e0), H], f"w1s_{e0}", S * (e1 - e0) * H)
+            load_scales(tile, w1_scales[e0:e1])
+            for e in range(e0, e1):
+                w1s[e] = tile[:, S * (e - e0) : S * (e - e0 + 1), :]
 
-        def load_w1(e, piece):
-            s0, s1 = WORD_LOADS[e][piece]
-            if piece == 0:
-                first_place[e] = used[0]
-            size = 4 * H if piece == 0 and e % 2 else 2 * H * (s1 - s0)
-            words = over_tokens([P, s1 - s0, 2 * H], f"w1_{e}_{s0}", size)
+        def load_w1(e, s0, s1):
+            if e == 0:
+                words = held([P, s1 - s0, 2 * H], U8, f"w1_{e}_{s0}")
+            elif (e, s0) == (E - 1, 0):
+                relu4_place.append(used[0])
+                words = over_tokens([P, s1 - s0, 2 * H], f"w1_{e}_{s0}", 4 * H)
+            else:
+                words = over_tokens([P, s1 - s0, 2 * H], f"w1_{e}_{s0}", 2 * H * (s1 - s0))
             nc.sync.dma_start(
                 out=words[:].bitcast(I32),
                 in_=w1_words[e, s0:s1].rearrange("s p b -> p s b").bitcast(I32),
@@ -97,14 +101,8 @@ def tile_moe_eps_mlp_relu2_kernel(
             for s in range(s0, s1):
                 w1[e, s] = words[:, s - s0, :]
 
-        def load_w2(e0):
-            words = over_tokens([P, 3, 2 * N], f"w2_{e0}", 6 * N)
-            nc.sync.dma_start(
-                out=words[:].bitcast(I32),
-                in_=w2_words[e0 : e0 + 3].rearrange("e s p b -> p (e s) b").bitcast(I32),
-            )
-            for e in range(e0, e0 + 3):
-                w2[e] = words[:, e - e0, :]
+        def move_plane(e0):
+            nc.sync.dma_start(out=planes[1, e0][0:112, :].bitcast(I32), in_=planes[0, e0][4 : 4 + 112, :].bitcast(I32))
 
         def cast(copy, s, c0, c1):
             copy(
@@ -139,64 +137,83 @@ def tile_moe_eps_mlp_relu2_kernel(
                 gb[e, s] = dst[:, C * (e - e0) : C * (e - e0 + 1)]
 
         tokens(0)
-        for e0 in (0, 3):
-            gather_words(0, e0, e0 + 3, 0)
+        for e0 in (0, 2):
+            gather_words(0, e0, e0 + 2, 0)
         tokens(1)
         for e0 in (0, 3):
-            nc.vector.tensor_copy(planes[0][:, C * e0 : C * (e0 + 3)], token_scales[:, 0:T].indirect(entries(e0, e0 + 3)))
+            nc.vector.tensor_copy(planes[0, e0][:], token_scales[:, 0:T].indirect(entries(e0, e0 + 3)))
         gather_words(1, 0, 2, 1)
         tokens(2)
         gather_words(2, 0, 2, 2)
         gather_bytes(2, 0, 2, 2)
+        gather_words(1, 2, 4, 2)
         tokens(3)
         for e in range(2):
             gather_words(3, e, e + 1, 3)
             gather_bytes(3, e, e + 1, 3)
         for e0 in (2, 4):
-            gather_words(1, e0, e0 + 2, 3)
+            if e0 == 4:
+                for s in range(2):
+                    gather_words(s, e0, e0 + 2, 3)
             gather_bytes(2, e0, e0 + 2, 3)
             for e in (e0, e0 + 1):
                 gather_words(2, e, e + 1, 3)
                 gather_words(3, e, e + 1, 3)
                 gather_bytes(3, e, e + 1, 3)
 
-        for e in range(E):
-            load_w1_scales(e)
-            for piece in range(len(WORD_LOADS[e])):
-                load_w1(e, piece)
-            if e == 0:
-                nc.sync.dma_start(out=planes[1][0:112, :].bitcast(I32), in_=planes[0][4 : 4 + 112, :].bitcast(I32))
+        load_w1(0, 0, S - 1)
+        load_w1_scales(0, 2)
+        move_plane(0)
+        load_w1_scales(2, 4)
+        load_w1(1, 0, S - 1)
+        both = over_tokens([P, 2, 2 * H], "w1_last_pass", 4 * H)
+        nc.sync.dma_start(
+            out=both[:].bitcast(I32), in_=w1_words[0:2, S - 1].rearrange("e p b -> p e b").bitcast(I32)
+        )
+        for e in range(2):
+            w1[e, S - 1] = both[:, e, :]
+        for s0, s1 in ((0, 2), (2, S)):
+            load_w1(2, s0, s1)
+        for s0, s1 in ((0, 2), (2, 3), (3, S)):
+            load_w1(3, s0, s1)
+        move_plane(3)
+        load_w1_scales(4, E)
+        for s0, s1 in ((0, 1), (1, S)):
+            load_w1(4, s0, s1)
+        for s0, s1 in ((0, 1), (1, 3), (3, S)):
+            load_w1(5, s0, s1)
+        w2 = over_tokens([P, E, 2 * N], "w2", 2 * E * N)
+        nc.sync.dma_start(out=w2[:].bitcast(I32), in_=w2_words.rearrange("e s p b -> p (e s) b").bitcast(I32))
         w2s = over_tokens([P, E, N], "w2s", E * N)
         load_scales(w2s, w2_scales)
-        load_w2(0)
-        load_w2(3)
 
         a, q = {}, {}
 
-        def product(e):
-            a[e] = bank(SUM_BANKS[e], f"a{e}")
-            for s in range(S):
-                plane = planes[s][:, C * e : C * (e + 1)] if s < 2 else gb[e, s]
+        def product(e, first=0, last=S):
+            if first == 0:
+                a[e] = bank(SUM_BANKS[e], f"a{e}")
+            passes = PASS_ORDER[e]
+            for s in passes[first:last]:
+                plane = planes[s, e // 3 * 3][:, C * (e % 3) : C * (e % 3 + 1)] if s < 2 else gb[e, s]
                 nc.tensor.matmul_mx(
                     out=a[e][:].rearrange("p d c -> p (d c)"),
                     lhsT=gw[e, s].bitcast(E4M3),
                     lhsT_scale=plane,
                     rhs=w1[e, s].bitcast(E2M1),
                     rhs_scale=w1s[e][:, s, :],
-                    start=(s == 0),
-                    stop=(s == S - 1),
+                    start=(s == passes[0]),
+                    stop=(s == passes[-1]),
                 )
 
         def relu(e):
-            if e % 2 == 0:
-                r = placed([P, 4, P], F32, f"r{e}", first_place[e + 1])
+            if e == 4:
+                r = placed([P, 4, P], F32, "r4", relu4_place[0])
             else:
-                r = held([P, 4, P], F32, f"r{e}")
+                r = held([P, 4, P], F32, f"r{e}", "gw1_2" if e == 2 else None)
             sums = a[e][:].rearrange("c u (v t) -> c t (u v)", t=4)
-            if e + 1 < E:
-                nc.scalar.activation(r[:], sums, RELU)
-            else:
-                nc.vector.tensor_scalar_max(r[:], sums, 0.0)
+            step = 2 if e in (3, 5) else 4
+            for d in range(0, 4, step):
+                nc.scalar.activation(r[:, d : d + step, :], sums[:, d : d + step, :], RELU)
             return r
 
         def turn(e, r):
@@ -214,7 +231,7 @@ def tile_moe_eps_mlp_relu2_kernel(
             hc, hs = q[e]
             nc.tensor.matmul_mx(
                 out=b,
-                lhsT=w2[e][:, 2 * P * n : 2 * P * (n + 1)].bitcast(E2M1),
+                lhsT=w2[:, e, 2 * P * n : 2 * P * (n + 1)].bitcast(E2M1),
                 lhsT_scale=w2s[:, e, P * n : P * (n + 1)],
                 rhs=hc[:].bitcast(E4M3),
                 rhs_scale=hs[:],
@@ -222,30 +239,31 @@ def tile_moe_eps_mlp_relu2_kernel(
                 stop=True,
             )
 
-        def results(copy, e0, banks):
-            for n in range(N // P):
-                b = bank(banks[n], f"y{e0}_{n}")
-                for e in range(e0, e0 + 3):
-                    second(e, n, b[:, e - e0, :])
-                copy(y[n][:, :, e0 : e0 + 3, :], b[:, 0:3, :].rearrange("p e (m u) -> p m e u", m=R))
+        def results(e0, e1, n, b, copy):
+            sums = bank(b, f"y{e0}_{n}")
+            for e in range(e0, e1):
+                second(e, n, sums[:, e - e0, :])
+            copy(y[n][:, :, e0:e1, :], sums[:, 0 : e1 - e0, :].rearrange("p e (m u) -> p m e u", m=R))
 
-        product(0)
-        product(1)
+        r = {}
+        for e in range(2):
+            product(e)
+        product(2, 0, 2)
         turn(0, relu(0))
-        product(2)
-        r = {1: relu(1)}
+        product(2, 2, S)
+        r[1] = relu(1)
         product(3)
         for e in (2, 3):
             r[e] = relu(e)
         for e in (1, 2, 3):
             turn(e, r[e])
-        product(4)
-        product(5)
+        for e in (4, 5):
+            product(e)
         for e in (4, 5):
             r[e] = relu(e)
         for e in (4, 5):
             turn(e, r[e])
-        results(nc.vector.tensor_copy, 0, (6, 7, 3))
-        results(nc.scalar.copy, 3, (4, 2, 0))
-        for n in range(N // P):
+        for n, (early, last) in enumerate(((4, 6), (2, 5), (0, 1))):
+            results(0, 4, n, early, nc.vector.tensor_copy if n == 0 else nc.scalar.copy)
+            results(4, E, n, last, nc.vector.tensor_copy)
             nc.sync.dma_start(out=out[P * n : P * (n + 1), :], in_=y[n][:].rearrange("p m e u -> p (m e u)"))

@@ -20,11 +20,6 @@ E2M1 = mybir.dt.float4_e2m1fn_x4
 RELU = mybir.ActivationFunctionType.Relu
 SQUARE = mybir.ActivationFunctionType.Square
 
-SCALAR_TOKENS = (192, 256, 512, 512)
-SUM_BANKS = (0, 1, 2, 3, 5, 6)
-TURN_BANKS = (4, 2, 0, 1, 7, 3)
-PASS_ORDER = (range(S), range(S), range(S), (1, 0, 2, 3), range(S), range(S))
-
 
 def tile_moe_eps_mlp_relu2_kernel(
     tc, xT, w1_words, w1_scales, w2_words, w2_scales, offs, out
@@ -32,7 +27,6 @@ def tile_moe_eps_mlp_relu2_kernel(
     nc = tc.nc
     with ExitStack() as ctx:
         keep = ctx.enter_context(tc.tile_pool(name="keep", bufs=1))
-        slab = ctx.enter_context(tc.tile_pool(name="slab", bufs=1))
         psum = ctx.enter_context(tc.psum_pool(name="psum", bufs=1))
 
         def bank(b, name):
@@ -41,25 +35,20 @@ def tile_moe_eps_mlp_relu2_kernel(
         def held(shape, dtype, name, tag=None):
             return keep.tile(shape, dtype, name=name, tag=tag or name, align_bytes=64)
 
-        def placed(shape, dtype, name, offset):
-            return slab.tile(shape, dtype, name=name, align_bytes=64, offset=offset)
-
-        used = [0]
-
-        def over_tokens(shape, name, size):
-            tile = placed(shape, U8, name, used[0])
-            used.append(used.pop() + size)
-            return tile
-
         offsets = keep.tile([P, SLOTS // 16], U16, name="offsets")
-        x = [placed([P, 4, T], F32, f"x{s}", 24 * T * s) for s in range(S)]
-        xg = [placed([P, T, 4], BF16, f"xg{s}", 24 * T * s + 16 * T) for s in range(S)]
+        x = [held([P, 4, T], F32, f"x{s}") for s in range(S)]
+        xg = [held([P, T, 4], BF16, f"xg{s}") for s in range(S)]
         codes = held([P, S * T], U32, "codes")
-        token_scales = held([P, 3 * T], U8, "token_scales")
+        packed = held([P, T], U8, "packed")
+        scales23 = held([P, 2 * T], U8, "scales23")
         planes = {(s, e0): held([P, 3 * C], U8, f"plane{s}_{e0}") for s in range(2) for e0 in (0, 3)}
+        runs = ((0, 2), (2, 4), (4, 6))
+        w1s = [held([P, S * (e1 - e0), H], U8, f"w1s_{e0}") for e0, e1 in runs]
+        w1_plane = {(e, s): w1s[i][:, S * (e - e0) + s, :] for i, (e0, e1) in enumerate(runs) for e in range(e0, e1) for s in range(S)}
+        w2s = held([P, E, N], U8, "w2s")
         y = [held([P, R, E, C // R], F32, f"y{n}") for n in range(N // P)]
         ident = held([P, P], F32, "ident")
-        w1, w1s, gw, gb, relu4_place = {}, {}, {}, {}, []
+        w1, gw, gb = {}, {}, {}
 
         def rows(s):
             return xT[512 * s : 512 * (s + 1), :].rearrange("(p j) w -> p j w", j=4)
@@ -69,8 +58,13 @@ def tile_moe_eps_mlp_relu2_kernel(
         for s in range(1, S):
             nc.sync.dma_start(out=x[s][:], in_=rows(s))
 
-        for plane in (token_scales, planes[1, 0], planes[1, 3]):
+        for i in (0, 1):
+            nc.vector.memset(w1s[i][:].rearrange("p a i -> p (a i)").bitcast(I32), 0)
+        for plane in (packed, scales23, planes[1, 0], planes[1, 3]):
             nc.vector.memset(plane[:].bitcast(I32), 0)
+        for i in (2,):
+            nc.gpsimd.memset(w1s[i][:].rearrange("p a i -> p (a i)").bitcast(I32), 0)
+        nc.vector.memset(w2s[:].rearrange("p a i -> p (a i)").bitcast(I32), 0)
         make_identity(nc, ident[:])
 
         def load_scales(tile, source):
@@ -80,20 +74,11 @@ def tile_moe_eps_mlp_relu2_kernel(
                     in_=source.rearrange("e s (b r) i -> r b (e s) i", r=4)[r].bitcast(I32),
                 )
 
-        def load_w1_scales(e0, e1):
-            tile = over_tokens([P, S * (e1 - e0), H], f"w1s_{e0}", S * (e1 - e0) * H)
-            load_scales(tile, w1_scales[e0:e1])
-            for e in range(e0, e1):
-                w1s[e] = tile[:, S * (e - e0) : S * (e - e0 + 1), :]
+        def load_w1_scales(i):
+            load_scales(w1s[i], w1_scales[runs[i][0] : runs[i][1]])
 
-        def load_w1(e, s0, s1):
-            if e == 0:
-                words = held([P, s1 - s0, 2 * H], U8, f"w1_{e}_{s0}")
-            elif (e, s0) == (E - 1, 0):
-                relu4_place.append(used[0])
-                words = over_tokens([P, s1 - s0, 2 * H], f"w1_{e}_{s0}", 4 * H)
-            else:
-                words = over_tokens([P, s1 - s0, 2 * H], f"w1_{e}_{s0}", 2 * H * (s1 - s0))
+        def load_w1(e, tag=None, s0=0, s1=S):
+            words = held([P, s1 - s0, 2 * H], U8, f"w1_{e}_{s0}", tag)
             nc.sync.dma_start(
                 out=words[:].bitcast(I32),
                 in_=w1_words[e, s0:s1].rearrange("s p b -> p s b").bitcast(I32),
@@ -101,131 +86,125 @@ def tile_moe_eps_mlp_relu2_kernel(
             for s in range(s0, s1):
                 w1[e, s] = words[:, s - s0, :]
 
-        def move_plane(e0):
-            nc.sync.dma_start(out=planes[1, e0][0:112, :].bitcast(I32), in_=planes[0, e0][4 : 4 + 112, :].bitcast(I32))
+        load_w1(0, None, 0, S - 1)
+        load_w1_scales(0)
 
-        def cast(copy, s, c0, c1):
+        def cast(copy, s, source, c0, c1):
             copy(
                 out=xg[s][:, c0:c1, :].rearrange("p (c i) j -> p c j i", i=4),
-                in_=x[s][:, :, c0:c1].rearrange("p j (c i) -> p c j i", i=4),
+                in_=source[:, :, c0:c1].rearrange("p j (c i) -> p c j i", i=4),
             )
 
-        def tokens(s):
-            cast(nc.scalar.copy, s, 0, SCALAR_TOKENS[s])
-            if SCALAR_TOKENS[s] < T:
-                cast(nc.vector.tensor_copy, s, SCALAR_TOKENS[s], T)
-            plane = token_scales[4 * s : P, 0:T] if s < 2 else token_scales[:, T * (s - 1) : T * s]
+        def quantize(s):
+            plane = packed[4 * s : P, :] if s < 2 else scales23[:, T * (s - 2) : T * (s - 1)]
             nc.vector.quantize_mx(
                 out=codes[:, T * s : T * (s + 1)].bitcast(E4M3),
                 scales=plane,
                 in_=xg[s][:].rearrange("p w j -> p (w j)"),
             )
 
-        def entries(e0, e1):
-            return offsets[:, C * e0 // 16 : C * e1 // 16]
+        def entries(j0, j1):
+            return offsets[:, j0 // 16 : j1 // 16]
 
         def gather_words(s, e0, e1, until):
             dst = held([P, C * (e1 - e0)], U32, f"gw{s}_{e0}")
-            nc.vector.tensor_copy(dst[:], codes[:, T * s : T * (until + 1)].indirect(entries(e0, e1)))
+            nc.vector.tensor_copy(dst[:], codes[:, T * s : T * (until + 1)].indirect(entries(C * e0, C * e1)))
             for e in range(e0, e1):
                 gw[e, s] = dst[:, C * (e - e0) : C * (e - e0 + 1)]
 
-        def gather_bytes(s, e0, e1, until):
+        def gather_bytes(s, e0, e1, window):
             dst = held([P, C * (e1 - e0)], U8, f"gb{s}_{e0}")
-            nc.vector.tensor_copy(dst[:], token_scales[:, T * (s - 1) : T * until].indirect(entries(e0, e1)))
+            nc.vector.tensor_copy(dst[:], window.indirect(entries(C * e0, C * e1)))
             for e in range(e0, e1):
                 gb[e, s] = dst[:, C * (e - e0) : C * (e - e0 + 1)]
 
-        tokens(0)
+        def tokens(s, split):
+            cast(nc.scalar.copy, s, x[s], 0, split)
+            if split < T:
+                cast(nc.vector.tensor_copy, s, x[s], split, T)
+            quantize(s)
+
+        def move_plane(e0):
+            nc.sync.dma_start(out=planes[1, e0][0:112, :].bitcast(I32), in_=planes[0, e0][4 : 4 + 112, :].bitcast(I32))
+
+        tokens(0, 192)
         for e0 in (0, 2):
             gather_words(0, e0, e0 + 2, 0)
-        tokens(1)
+        tokens(1, 256)
         for e0 in (0, 3):
-            nc.vector.tensor_copy(planes[0, e0][:], token_scales[:, 0:T].indirect(entries(e0, e0 + 3)))
+            nc.vector.tensor_copy(planes[0, e0][:], packed[:].indirect(entries(C * e0, C * (e0 + 3))))
+        move_plane(0)
+        load_w1_scales(1)
         gather_words(1, 0, 2, 1)
-        tokens(2)
+        tokens(2, T)
         gather_words(2, 0, 2, 2)
-        gather_bytes(2, 0, 2, 2)
+        gather_bytes(2, 0, 2, scales23[:, 0:T])
         gather_words(1, 2, 4, 2)
-        tokens(3)
+        tokens(3, T)
         for e in range(2):
             gather_words(3, e, e + 1, 3)
-            gather_bytes(3, e, e + 1, 3)
+            gather_bytes(3, e, e + 1, scales23[:, T : 2 * T])
         for e0 in (2, 4):
-            if e0 == 4:
-                for s in range(2):
-                    gather_words(s, e0, e0 + 2, 3)
-            gather_bytes(2, e0, e0 + 2, 3)
+            gather_bytes(2, e0, e0 + 2, scales23[:])
             for e in (e0, e0 + 1):
                 gather_words(2, e, e + 1, 3)
+                if e == 4:
+                    gather_words(0, e0, e0 + 2, 3)
+                    gather_words(1, e0, e0 + 2, 3)
                 gather_words(3, e, e + 1, 3)
-                gather_bytes(3, e, e + 1, 3)
+                gather_bytes(3, e, e + 1, scales23[:, T : 2 * T])
 
-        load_w1(0, 0, S - 1)
-        load_w1_scales(0, 2)
-        move_plane(0)
-        load_w1_scales(2, 4)
-        load_w1(1, 0, S - 1)
-        both = over_tokens([P, 2, 2 * H], "w1_last_pass", 4 * H)
+        load_w1(1, "x0", 0, S - 1)
+        both = held([P, 2, 2 * H], U8, "w1_last_pass", "xg0")
         nc.sync.dma_start(
             out=both[:].bitcast(I32), in_=w1_words[0:2, S - 1].rearrange("e p b -> p e b").bitcast(I32)
         )
         for e in range(2):
             w1[e, S - 1] = both[:, e, :]
-        for s0, s1 in ((0, 2), (2, S)):
-            load_w1(2, s0, s1)
-        for s0, s1 in ((0, 2), (2, 3), (3, S)):
-            load_w1(3, s0, s1)
+        load_w1(2, "x1", 0, 2)
+        load_w1(2, "xg1", 2, S)
+        load_w1(3, "packed", 0, 2)
+        load_w1(3, "x2", 2, 3)
+        load_w1(3, "xg2", 3, S)
         move_plane(3)
-        load_w1_scales(4, E)
-        for s0, s1 in ((0, 1), (1, S)):
-            load_w1(4, s0, s1)
-        for s0, s1 in ((0, 1), (1, 3), (3, S)):
-            load_w1(5, s0, s1)
-        w2 = over_tokens([P, E, 2 * N], "w2", 2 * E * N)
-        nc.sync.dma_start(out=w2[:].bitcast(I32), in_=w2_words.rearrange("e s p b -> p (e s) b").bitcast(I32))
-        w2s = over_tokens([P, E, N], "w2s", E * N)
-        load_scales(w2s, w2_scales)
+        load_w1_scales(2)
+        load_w1(4, "x3", 0, 1)
 
-        a, q = {}, {}
-
-        def product(e, first=0, last=S):
-            if first == 0:
-                a[e] = bank(SUM_BANKS[e], f"a{e}")
-            passes = PASS_ORDER[e]
-            for s in passes[first:last]:
+        def first(e, a, order, passes):
+            for s in passes:
                 plane = planes[s, e // 3 * 3][:, C * (e % 3) : C * (e % 3 + 1)] if s < 2 else gb[e, s]
                 nc.tensor.matmul_mx(
-                    out=a[e][:].rearrange("p d c -> p (d c)"),
+                    out=a[:].rearrange("p d c -> p (d c)"),
                     lhsT=gw[e, s].bitcast(E4M3),
                     lhsT_scale=plane,
                     rhs=w1[e, s].bitcast(E2M1),
-                    rhs_scale=w1s[e][:, s, :],
-                    start=(s == passes[0]),
-                    stop=(s == passes[-1]),
+                    rhs_scale=w1_plane[e, s],
+                    start=(s == order[0]),
+                    stop=(s == order[-1]),
                 )
 
-        def relu(e):
-            if e == 4:
-                r = placed([P, 4, P], F32, "r4", relu4_place[0])
-            else:
-                r = held([P, 4, P], F32, f"r{e}", "gw1_2" if e == 2 else None)
-            sums = a[e][:].rearrange("c u (v t) -> c t (u v)", t=4)
-            step = 2 if e in (3, 5) else 4
+        def relu(e, a):
+            r = held([P, 4, P], F32, f"r{e}", {2: "gw1_2", 4: "plane0_0"}.get(e))
+            step = 2 if e in (3, E - 1) else 4
             for d in range(0, 4, step):
-                nc.scalar.activation(r[:, d : d + step, :], sums[:, d : d + step, :], RELU)
+                nc.scalar.activation(r[:, d : d + step, :], a[:].rearrange("c u (v t) -> c t (u v)", t=4)[:, d : d + step, :], RELU)
             return r
 
-        def turn(e, r):
-            t = bank(TURN_BANKS[e], f"t{e}")
+        def turn(r, t):
             for d in range(4):
                 nc.tensor.transpose(t[:, d, :], r[:, d, :], ident[:])
+            return t
+
+        def square(e, t):
             h = held([P, C, 4], BF16, f"h{e}")
             nc.scalar.activation(h[:], t[:].rearrange("p t c -> p c t"), SQUARE)
+            return h
+
+        def quantize_h(e, h):
             hc = held([P, C], U32, f"hc{e}")
             hs = held([P, C], U8, f"hs{e}")
             nc.vector.quantize_mx(out=hc[:].bitcast(E4M3), scales=hs[:], in_=h[:].rearrange("p c t -> p (c t)"))
-            q[e] = hc, hs
+            return hc, hs
 
         def second(e, n, b):
             hc, hs = q[e]
@@ -245,24 +224,40 @@ def tile_moe_eps_mlp_relu2_kernel(
                 second(e, n, sums[:, e - e0, :])
             copy(y[n][:, :, e0:e1, :], sums[:, 0 : e1 - e0, :].rearrange("p e (m u) -> p m e u", m=R))
 
-        r = {}
-        for e in range(2):
-            product(e)
-        product(2, 0, 2)
-        turn(0, relu(0))
-        product(2, 2, S)
-        r[1] = relu(1)
-        product(3)
+        a, r, q = {}, {}, {}
+
+        def product(e, b, order, passes=None):
+            a[e] = bank(b, f"a{e}")
+            first(e, a[e], order, passes or order)
+
+        def finish(e, b):
+            q[e] = quantize_h(e, square(e, turn(r[e], bank(b, f"t{e}"))))
+
+        product(0, 0, range(S))
+        product(1, 1, range(S))
+        product(2, 2, range(S), (0, 1))
+        r[0] = relu(0, a[0])
+        finish(0, 4)
+        first(2, a[2], range(S), (2, 3))
+        r[1] = relu(1, a[1])
+        load_w1(4, "x0", 1, S)
+        load_w1(5, "plane0_0", 0, 1)
+        load_w1(5, "xg0", 1, 3)
+        load_w1(5, "x1", 3, S)
+        w2 = held([P, E, 2 * N], U8, "w2", "xg3")
+        nc.sync.dma_start(out=w2[:].bitcast(I32), in_=w2_words.rearrange("e s p b -> p (e s) b").bitcast(I32))
+        load_scales(w2s, w2_scales)
+        product(3, 3, (1, 0, 2, 3))
         for e in (2, 3):
-            r[e] = relu(e)
-        for e in (1, 2, 3):
-            turn(e, r[e])
+            r[e] = relu(e, a[e])
+        for e, b in ((1, 2), (2, 0), (3, 1)):
+            finish(e, b)
+        product(4, 5, range(S))
+        product(5, 6, range(S))
         for e in (4, 5):
-            product(e)
-        for e in (4, 5):
-            r[e] = relu(e)
-        for e in (4, 5):
-            turn(e, r[e])
+            r[e] = relu(e, a[e])
+        for e, b in ((4, 7), (5, 3)):
+            finish(e, b)
         for n, (early, last) in enumerate(((4, 6), (2, 5), (0, 1))):
             results(0, 4, n, early, nc.vector.tensor_copy if n == 0 else nc.scalar.copy)
             results(4, E, n, last, nc.vector.tensor_copy)

@@ -19,6 +19,7 @@ E4M3 = mybir.dt.float8_e4m3fn_x4
 E2M1 = mybir.dt.float4_e2m1fn_x4
 RELU = mybir.ActivationFunctionType.Relu
 SQUARE = mybir.ActivationFunctionType.Square
+MULT = mybir.AluOpType.mult
 
 
 def tile_moe_eps_mlp_relu2_kernel(
@@ -185,10 +186,24 @@ def tile_moe_eps_mlp_relu2_kernel(
 
         def relu(e, a):
             r = held([P, 4, P], F32, f"r{e}", {2: "gw1_2", 4: "plane0_0"}.get(e))
-            step = 2 if e in (3, E - 1) else 4
+            step = 2 if e == E - 1 else 4
             for d in range(0, 4, step):
                 nc.scalar.activation(r[:, d : d + step, :], a[:].rearrange("c u (v t) -> c t (u v)", t=4)[:, d : d + step, :], RELU)
             return r
+
+        def relu_pairs(e, a):
+            r = held([P, 2, P, 2], F32, f"r{e}", {4: "plane0_0"}.get(e))
+            nc.scalar.activation(
+                r[:], a[:].rearrange("c d f -> c (d f)").rearrange("c (p u v) -> c u p v", u=2, v=2), RELU
+            )
+            return r[:].rearrange("c u p v -> c (u p v)")
+
+        def turn_pairs(e, g, t):
+            for u in range(2):
+                nc.tensor.transpose(t[:, u, :], g[:].bitcast(F32)[:, P * u : P * (u + 1)], ident[:])
+            h = held([P, C, 4], BF16, f"h{e}")
+            nc.vector.tensor_copy(h[:].bitcast(F32), t[:, 0:2, :].rearrange("p u c -> p c u"))
+            return h
 
         def turn(r, t):
             for d in range(4):
@@ -248,17 +263,23 @@ def tile_moe_eps_mlp_relu2_kernel(
         nc.sync.dma_start(out=w2[:].bitcast(I32), in_=w2_words.rearrange("e s p b -> p (e s) b").bitcast(I32))
         load_scales(w2s, w2_scales)
         product(3, 3, (1, 0, 2, 3))
-        for e in (2, 3):
-            r[e] = relu(e, a[e])
-        for e, b in ((1, 2), (2, 0), (3, 1)):
+        r[2] = relu(2, a[2])
+        r[3] = relu_pairs(3, a[3])
+        for e, b in ((1, 2), (2, 0)):
             finish(e, b)
+        g3 = held([P, H], BF16, "g3")
+        nc.scalar.activation(g3[:], r[3], SQUARE)
         product(4, 5, range(S))
         product(5, 6, range(S))
-        for e in (4, 5):
-            r[e] = relu(e, a[e])
-        for e, b in ((4, 7), (5, 3)):
-            finish(e, b)
-        for n, (early, last) in enumerate(((4, 6), (2, 5), (0, 1))):
+        r[4] = relu_pairs(4, a[4])
+        g4 = held([P, H], BF16, "g4")
+        nc.vector.tensor_tensor(g4[:], r[4], r[4], MULT)
+        r[5] = relu(5, a[5])
+        q[3] = quantize_h(3, turn_pairs(3, g3, bank(5, "t3")))
+        t5 = turn(r[5], bank(3, "t5"))
+        q[4] = quantize_h(4, turn_pairs(4, g4, bank(7, "t4")))
+        q[5] = quantize_h(5, square(5, t5))
+        for n, (early, last) in enumerate(((6, 4), (5, 2), (7, 0))):
             results(0, 4, n, early, nc.vector.tensor_copy if n == 0 else nc.scalar.copy)
             results(4, E, n, last, nc.vector.tensor_copy)
             nc.sync.dma_start(out=out[P * n : P * (n + 1), :], in_=y[n][:].rearrange("p m e u -> p (m e u)"))

@@ -169,7 +169,7 @@ def tile_moe_eps_mlp_relu2_kernel(
         load_w1(3, "xg2", 3, S)
         move_plane(3)
         load_w1_scales(2)
-        load_w1(4, "x3", 0, 1)
+        load_w1(4, "x3", 0, 2)
 
         def first(e, a, order, passes):
             for s in passes:
@@ -185,25 +185,26 @@ def tile_moe_eps_mlp_relu2_kernel(
                 )
 
         def relu(e, a):
-            r = held([P, 4, P], F32, f"r{e}", {2: "gw1_2", 4: "plane0_0"}.get(e))
+            r = held([P, 4, P], F32, f"r{e}", {2: "gw1_2"}.get(e))
             step = 2 if e == E - 1 else 4
             for d in range(0, 4, step):
                 nc.scalar.activation(r[:, d : d + step, :], a[:].rearrange("c u (v t) -> c t (u v)", t=4)[:, d : d + step, :], RELU)
             return r
 
         def relu_pairs(e, a):
-            r = held([P, 2, P, 2], F32, f"r{e}", {4: "plane0_0"}.get(e))
+            r = held([P, 2, P, 2], F32, f"r{e}", None)
             nc.scalar.activation(
                 r[:], a[:].rearrange("c d f -> c (d f)").rearrange("c (p u v) -> c u p v", u=2, v=2), RELU
             )
             return r[:].rearrange("c u p v -> c (u p v)")
 
-        def turn_pairs(e, g, t):
-            for u in range(2):
-                nc.tensor.transpose(t[:, u, :], g[:].bitcast(F32)[:, P * u : P * (u + 1)], ident[:])
-            h = held([P, C, 4], BF16, f"h{e}")
-            nc.vector.tensor_copy(h[:].bitcast(F32), t[:, 0:2, :].rearrange("p u c -> p c u"))
-            return h
+        def square_pairs(e, r):
+            g = held([P, H], BF16, f"g{e}", "gw1_2" if e == 3 else None)
+            if e == E - 2:
+                nc.vector.tensor_tensor(g[:], r, r, MULT)
+            else:
+                nc.scalar.activation(g[:], r, SQUARE)
+            return g
 
         def turn(r, t):
             for d in range(4):
@@ -219,7 +220,7 @@ def tile_moe_eps_mlp_relu2_kernel(
             hc = held([P, C], U32, f"hc{e}")
             hs = held([P, C], U8, f"hs{e}")
             nc.vector.quantize_mx(out=hc[:].bitcast(E4M3), scales=hs[:], in_=h[:].rearrange("p c t -> p (c t)"))
-            return hc, hs
+            return hc[:], hs[:]
 
         def second(e, n, b):
             hc, hs = q[e]
@@ -227,8 +228,8 @@ def tile_moe_eps_mlp_relu2_kernel(
                 out=b,
                 lhsT=w2[:, e, 2 * P * n : 2 * P * (n + 1)].bitcast(E2M1),
                 lhsT_scale=w2s[:, e, P * n : P * (n + 1)],
-                rhs=hc[:].bitcast(E4M3),
-                rhs_scale=hs[:],
+                rhs=hc.bitcast(E4M3),
+                rhs_scale=hs,
                 start=True,
                 stop=True,
             )
@@ -255,9 +256,9 @@ def tile_moe_eps_mlp_relu2_kernel(
         finish(0, 4)
         first(2, a[2], range(S), (2, 3))
         r[1] = relu(1, a[1])
-        load_w1(4, "x0", 1, S)
-        load_w1(5, "plane0_0", 0, 1)
-        load_w1(5, "xg0", 1, 3)
+        load_w1(4, "x0", 2, S)
+        load_w1(5, "plane0_0", 0, 2)
+        load_w1(5, "xg0", 2, 3)
         load_w1(5, "x1", 3, S)
         w2 = held([P, E, 2 * N], U8, "w2", "xg3")
         nc.sync.dma_start(out=w2[:].bitcast(I32), in_=w2_words.rearrange("e s p b -> p (e s) b").bitcast(I32))
@@ -267,19 +268,32 @@ def tile_moe_eps_mlp_relu2_kernel(
         r[3] = relu_pairs(3, a[3])
         for e, b in ((1, 2), (2, 0)):
             finish(e, b)
-        g3 = held([P, H], BF16, "g3")
-        nc.scalar.activation(g3[:], r[3], SQUARE)
+        g = {3: square_pairs(3, r[3])}
         product(4, 5, range(S))
-        product(5, 6, range(S))
-        r[4] = relu_pairs(4, a[4])
-        g4 = held([P, H], BF16, "g4")
-        nc.vector.tensor_tensor(g4[:], r[4], r[4], MULT)
+        product(5, 0, range(S))
+        g[4] = square_pairs(4, relu_pairs(4, a[4]))
         r[5] = relu(5, a[5])
-        q[3] = quantize_h(3, turn_pairs(3, g3, bank(5, "t3")))
+        t34 = bank(7, "t34")
+        for e in (4, 3):
+            for u in range(2):
+                nc.tensor.transpose(t34[:, 2 * (e - 3) + u, :], g[e][:].bitcast(F32)[:, P * u : P * (u + 1)], ident[:])
         t5 = turn(r[5], bank(3, "t5"))
-        q[4] = quantize_h(4, turn_pairs(4, g4, bank(7, "t4")))
+        h34 = held([P, 8 * C], BF16, "h34")
+        nc.vector.tensor_copy(
+            h34[:].bitcast(F32).rearrange("p (e c u) -> p e c u", u=2, c=C),
+            t34[:].rearrange("p (e u) c -> p e c u", u=2),
+        )
+        hc34 = held([P, 2 * C], U32, "hc34")
+        hs34 = held([P, 2 * C], U8, "hs34")
+        nc.vector.quantize_mx(out=hc34[:].bitcast(E4M3), scales=hs34[:], in_=h34[:])
+        for e in (3, 4):
+            q[e] = hc34[:, C * (e - 3) : C * (e - 2)], hs34[:, C * (e - 3) : C * (e - 2)]
         q[5] = quantize_h(5, square(5, t5))
-        for n, (early, last) in enumerate(((6, 4), (5, 2), (7, 0))):
-            results(0, 4, n, early, nc.vector.tensor_copy if n == 0 else nc.scalar.copy)
-            results(4, E, n, last, nc.vector.tensor_copy)
+        results(0, 3, 0, 0, nc.scalar.copy)
+        results(3, 5, 0, 4, nc.scalar.copy)
+        results(5, E, 0, 2, nc.vector.tensor_copy)
+        nc.sync.dma_start(out=out[0:P, :], in_=y[0][:].rearrange("p m e u -> p (m e u)"))
+        for n, early, last in ((1, 7, 6), (2, 3, 1)):
+            results(0, 4, n, early, nc.scalar.copy if n == 2 else nc.vector.tensor_copy)
+            results(4, E, n, last, nc.scalar.copy if n == 1 else nc.vector.tensor_copy)
             nc.sync.dma_start(out=out[P * n : P * (n + 1), :], in_=y[n][:].rearrange("p m e u -> p (m e u)"))

@@ -34,7 +34,7 @@ def tile_moe_eps_mlp_relu2_kernel(
             return psum.tile([P, 4, C], F32, name=name, tag=f"bank{b}")
 
         def held(shape, dtype, name, tag=None):
-            return keep.tile(shape, dtype, name=name, tag=tag or name, align_bytes=64)
+            return keep.tile(shape, dtype, name=name, tag=tag or name, align_bytes=256)
 
         offsets = keep.tile([P, SLOTS // 16], U16, name="offsets")
         x = [held([P, 4, T], F32, f"x{s}") for s in range(S)]

from contextlib import ExitStack

import concourse.mybir as mybir
from concourse.masks import make_identity

K, T, E, C, H, N, R = 2048, 512, 6, 128, 512, 384, 4
P = 128
S = K // 512
SLOTS = E * C
FLOPS = 2 * SLOTS * (K * H + H * N)

F32 = mybir.dt.float32
BF16 = mybir.dt.bfloat16
U32 = mybir.dt.uint32
I32 = mybir.dt.int32
U16 = mybir.dt.uint16
U8 = mybir.dt.uint8
E4M3 = mybir.dt.float8_e4m3fn_x4
E2M1 = mybir.dt.float4_e2m1fn_x4
RELU = mybir.ActivationFunctionType.Relu
SQUARE = mybir.ActivationFunctionType.Square
MULT = mybir.AluOpType.mult


def tile_moe_eps_mlp_relu2_kernel(
    tc, xT, w1_words, w1_scales, w2_words, w2_scales, offs, out
):
    nc = tc.nc
    with ExitStack() as ctx:
        keep = ctx.enter_context(tc.tile_pool(name="keep", bufs=1))
        psum = ctx.enter_context(tc.psum_pool(name="psum", bufs=1))

        def bank(b, name):
            return psum.tile([P, 4, C], F32, name=name, tag=f"bank{b}")

        def held(shape, dtype, name, tag=None):
            return keep.tile(shape, dtype, name=name, tag=tag or name, align_bytes=256)

        offsets = keep.tile([P, SLOTS // 16], U16, name="offsets")
        x = [held([P, 4, T], F32, f"x{s}") for s in range(S)]
        xg = [held([P, T, 4], BF16, f"xg{s}") for s in range(S)]
        codes = held([P, S * T], U32, "codes")
        packed = held([P, T], U8, "packed")
        scales23 = held([P, 2 * T], U8, "scales23")
        planes = {(s, e0): held([P, 3 * C], U8, f"plane{s}_{e0}") for s in range(2) for e0 in (0, 3)}
        runs = ((0, 2), (2, 4), (4, 6))
        w1s = [held([P, S * (e1 - e0), H], U8, f"w1s_{e0}") for e0, e1 in runs]
        w1_plane = {(e, s): w1s[i][:, S * (e - e0) + s, :] for i, (e0, e1) in enumerate(runs) for e in range(e0, e1) for s in range(S)}
        w2s = held([P, E, N], U8, "w2s")
        y = [held([P, R, E, C // R], F32, f"y{n}") for n in range(N // P)]
        ident = held([P, P], F32, "ident")
        w1, gw, gb = {}, {}, {}

        def rows(s):
            return xT[512 * s : 512 * (s + 1), :].rearrange("(p j) w -> p j w", j=4)

        nc.sync.dma_start(out=x[0][:], in_=rows(0))
        nc.sync.dma_start(offsets[:], offs)
        for s in range(1, S):
            nc.sync.dma_start(out=x[s][:], in_=rows(s))

        for i in (0, 1):
            nc.vector.memset(w1s[i][:].rearrange("p a i -> p (a i)").bitcast(I32), 0)
        for plane in (packed, scales23, planes[1, 0], planes[1, 3]):
            nc.vector.memset(plane[:].bitcast(I32), 0)
        for i in (2,):
            nc.gpsimd.memset(w1s[i][:].rearrange("p a i -> p (a i)").bitcast(I32), 0)
        nc.vector.memset(w2s[:].rearrange("p a i -> p (a i)").bitcast(I32), 0)
        make_identity(nc, ident[:])

        def load_scales(tile, source):
            for r in range(4):
                nc.sync.dma_start(
                    out=tile[r:P:32, :, :].bitcast(I32),
                    in_=source.rearrange("e s (b r) i -> r b (e s) i", r=4)[r].bitcast(I32),
                )

        def load_w1_scales(i):
            load_scales(w1s[i], w1_scales[runs[i][0] : runs[i][1]])

        def load_w1(e, tag=None, s0=0, s1=S):
            words = held([P, s1 - s0, 2 * H], U8, f"w1_{e}_{s0}", tag)
            nc.sync.dma_start(
                out=words[:].bitcast(I32),
                in_=w1_words[e, s0:s1].rearrange("s p b -> p s b").bitcast(I32),
            )
            for s in range(s0, s1):
                w1[e, s] = words[:, s - s0, :]

        load_w1(0, None, 0, S - 1)
        load_w1_scales(0)

        def cast(copy, s, source, c0, c1):
            copy(
                out=xg[s][:, c0:c1, :].rearrange("p (c i) j -> p c j i", i=4),
                in_=source[:, :, c0:c1].rearrange("p j (c i) -> p c j i", i=4),
            )

        def quantize(s):
            plane = packed[4 * s : P, :] if s < 2 else scales23[:, T * (s - 2) : T * (s - 1)]
            nc.vector.quantize_mx(
                out=codes[:, T * s : T * (s + 1)].bitcast(E4M3),
                scales=plane,
                in_=xg[s][:].rearrange("p w j -> p (w j)"),
            )

        def entries(j0, j1):
            return offsets[:, j0 // 16 : j1 // 16]

        def gather_words(s, e0, e1, until):
            dst = held([P, C * (e1 - e0)], U32, f"gw{s}_{e0}")
            nc.vector.tensor_copy(dst[:], codes[:, T * s : T * (until + 1)].indirect(entries(C * e0, C * e1)))
            for e in range(e0, e1):
                gw[e, s] = dst[:, C * (e - e0) : C * (e - e0 + 1)]

        def gather_bytes(s, e0, e1, window):
            dst = held([P, C * (e1 - e0)], U8, f"gb{s}_{e0}")
            nc.vector.tensor_copy(dst[:], window.indirect(entries(C * e0, C * e1)))
            for e in range(e0, e1):
                gb[e, s] = dst[:, C * (e - e0) : C * (e - e0 + 1)]

        def tokens(s, split):
            cast(nc.scalar.copy, s, x[s], 0, split)
            if split < T:
                cast(nc.vector.tensor_copy, s, x[s], split, T)
            quantize(s)

        def move_plane(e0):
            nc.sync.dma_start(out=planes[1, e0][0:112, :].bitcast(I32), in_=planes[0, e0][4 : 4 + 112, :].bitcast(I32))

        tokens(0, 192)
        for e0 in (0, 2):
            gather_words(0, e0, e0 + 2, 0)
        tokens(1, 256)
        for e0 in (0, 3):
            nc.vector.tensor_copy(planes[0, e0][:], packed[:].indirect(entries(C * e0, C * (e0 + 3))))
        move_plane(0)
        load_w1_scales(1)
        gather_words(1, 0, 2, 1)
        tokens(2, T)
        gather_words(2, 0, 2, 2)
        gather_bytes(2, 0, 2, scales23[:, 0:T])
        gather_words(1, 2, 4, 2)
        tokens(3, T)
        for e in range(2):
            gather_words(3, e, e + 1, 3)
            gather_bytes(3, e, e + 1, scales23[:, T : 2 * T])
        for e0 in (2, 4):
            gather_bytes(2, e0, e0 + 2, scales23[:])
            for e in (e0, e0 + 1):
                gather_words(2, e, e + 1, 3)
                if e == 4:
                    gather_words(0, e0, e0 + 2, 3)
                    gather_words(1, e0, e0 + 2, 3)
                gather_words(3, e, e + 1, 3)
                gather_bytes(3, e, e + 1, scales23[:, T : 2 * T])

        load_w1(1, "x0", 0, S - 1)
        both = held([P, 2, 2 * H], U8, "w1_last_pass", "xg0")
        nc.sync.dma_start(
            out=both[:].bitcast(I32), in_=w1_words[0:2, S - 1].rearrange("e p b -> p e b").bitcast(I32)
        )
        for e in range(2):
            w1[e, S - 1] = both[:, e, :]
        load_w1(2, "x1", 0, 2)
        load_w1(2, "xg1", 2, S)
        load_w1(3, "packed", 0, 2)
        load_w1(3, "x2", 2, 3)
        load_w1(3, "xg2", 3, S)
        move_plane(3)
        load_w1_scales(2)
        load_w1(4, "x3", 0, 2)

        def first(e, a, order, passes):
            for s in passes:
                plane = planes[s, e // 3 * 3][:, C * (e % 3) : C * (e % 3 + 1)] if s < 2 else gb[e, s]
                nc.tensor.matmul_mx(
                    out=a[:].rearrange("p d c -> p (d c)"),
                    lhsT=gw[e, s].bitcast(E4M3),
                    lhsT_scale=plane,
                    rhs=w1[e, s].bitcast(E2M1),
                    rhs_scale=w1_plane[e, s],
                    start=(s == order[0]),
                    stop=(s == order[-1]),
                )

        def relu(e, a):
            r = held([P, 4, P], F32, f"r{e}", {2: "gw1_2"}.get(e))
            step = 2 if e == E - 1 else 4
            for d in range(0, 4, step):
                nc.scalar.activation(r[:, d : d + step, :], a[:].rearrange("c u (v t) -> c t (u v)", t=4)[:, d : d + step, :], RELU)
            return r

        def relu_pairs(e, a):
            r = held([P, 2, P, 2], F32, f"r{e}", None)
            nc.scalar.activation(
                r[:], a[:].rearrange("c d f -> c (d f)").rearrange("c (p u v) -> c u p v", u=2, v=2), RELU
            )
            return r[:].rearrange("c u p v -> c (u p v)")

        def square_pairs(e, r):
            g = held([P, H], BF16, f"g{e}", "gw1_2" if e == 3 else None)
            if e == E - 2:
                nc.vector.tensor_tensor(g[:], r, r, MULT)
            else:
                nc.scalar.activation(g[:], r, SQUARE)
            return g

        def turn(r, t):
            for d in range(4):
                nc.tensor.transpose(t[:, d, :], r[:, d, :], ident[:])
            return t

        def square(e, t):
            h = held([P, C, 4], BF16, f"h{e}")
            nc.scalar.activation(h[:], t[:].rearrange("p t c -> p c t"), SQUARE)
            return h

        def quantize_h(e, h):
            hc = held([P, C], U32, f"hc{e}")
            hs = held([P, C], U8, f"hs{e}")
            nc.vector.quantize_mx(out=hc[:].bitcast(E4M3), scales=hs[:], in_=h[:].rearrange("p c t -> p (c t)"))
            return hc[:], hs[:]

        def second(e, n, b):
            hc, hs = q[e]
            nc.tensor.matmul_mx(
                out=b,
                lhsT=w2[:, e, 2 * P * n : 2 * P * (n + 1)].bitcast(E2M1),
                lhsT_scale=w2s[:, e, P * n : P * (n + 1)],
                rhs=hc.bitcast(E4M3),
                rhs_scale=hs,
                start=True,
                stop=True,
            )

        def results(e0, e1, n, b, copy):
            sums = bank(b, f"y{e0}_{n}")
            for e in range(e0, e1):
                second(e, n, sums[:, e - e0, :])
            copy(y[n][:, :, e0:e1, :], sums[:, 0 : e1 - e0, :].rearrange("p e (m u) -> p m e u", m=R))

        a, r, q = {}, {}, {}

        def product(e, b, order, passes=None):
            a[e] = bank(b, f"a{e}")
            first(e, a[e], order, passes or order)

        def finish(e, b):
            q[e] = quantize_h(e, square(e, turn(r[e], bank(b, f"t{e}"))))

        product(0, 0, range(S))
        product(1, 1, range(S))
        product(2, 2, range(S), (0, 1))
        r[0] = relu(0, a[0])
        finish(0, 4)
        first(2, a[2], range(S), (2, 3))
        r[1] = relu(1, a[1])
        load_w1(4, "x0", 2, S)
        load_w1(5, "plane0_0", 0, 2)
        load_w1(5, "xg0", 2, 3)
        load_w1(5, "x1", 3, S)
        w2 = held([P, E, 2 * N], U8, "w2", "xg3")
        nc.sync.dma_start(out=w2[:].bitcast(I32), in_=w2_words.rearrange("e s p b -> p (e s) b").bitcast(I32))
        load_scales(w2s, w2_scales)
        product(3, 3, (1, 0, 2, 3))
        r[2] = relu(2, a[2])
        r[3] = relu_pairs(3, a[3])
        for e, b in ((1, 2), (2, 0)):
            finish(e, b)
        g = {3: square_pairs(3, r[3])}
        product(4, 5, range(S))
        product(5, 0, range(S))
        g[4] = square_pairs(4, relu_pairs(4, a[4]))
        r[5] = relu(5, a[5])
        t34 = bank(7, "t34")
        for e in (4, 3):
            for u in range(2):
                nc.tensor.transpose(t34[:, 2 * (e - 3) + u, :], g[e][:].bitcast(F32)[:, P * u : P * (u + 1)], ident[:])
        t5 = turn(r[5], bank(3, "t5"))
        h34 = held([P, 8 * C], BF16, "h34")
        nc.vector.tensor_copy(
            h34[:].bitcast(F32).rearrange("p (e c u) -> p e c u", u=2, c=C),
            t34[:].rearrange("p (e u) c -> p e c u", u=2),
        )
        hc34 = held([P, 2 * C], U32, "hc34")
        hs34 = held([P, 2 * C], U8, "hs34")
        nc.vector.quantize_mx(out=hc34[:].bitcast(E4M3), scales=hs34[:], in_=h34[:])
        for e in (3, 4):
            q[e] = hc34[:, C * (e - 3) : C * (e - 2)], hs34[:, C * (e - 3) : C * (e - 2)]
        q[5] = quantize_h(5, square(5, t5))
        results(0, 3, 0, 0, nc.scalar.copy)
        results(3, 5, 0, 4, nc.scalar.copy)
        results(5, E, 0, 2, nc.vector.tensor_copy)
        nc.sync.dma_start(out=out[0:P, :], in_=y[0][:].rearrange("p m e u -> p (m e u)"))
        for n, early, last in ((1, 7, 6), (2, 3, 1)):
            results(0, 4, n, early, nc.scalar.copy if n == 2 else nc.vector.tensor_copy)
            results(4, E, n, last, nc.scalar.copy if n == 1 else nc.vector.tensor_copy)
            nc.sync.dma_start(out=out[P * n : P * (n + 1), :], in_=y[n][:].rearrange("p m e u -> p (m e u)"))
